import numpy as np
import ml_dtypes


def mxq(x, axis, fmt="e4m3"):
    dtype, down = {"e4m3": (ml_dtypes.float8_e4m3fn, 7), "e5m2": (ml_dtypes.float8_e5m2, 14)}[fmt]
    v = np.moveaxis(np.asarray(x, np.float32).astype(ml_dtypes.bfloat16).astype(np.float64), axis, -1)
    blocks = v.reshape(v.shape[:-1] + (-1, 32))
    amax = np.abs(blocks).max(-1, keepdims=True)
    byte = np.maximum(np.where(amax > 0, np.frexp(amax)[1] - 1 + 127, 0) - down, 1)
    scale = np.exp2(byte - 127.0)
    codes = (blocks / scale).astype(np.float32).astype(dtype).astype(np.float64)
    return np.moveaxis((codes * scale).reshape(v.shape), -1, axis)


WIDE = False


def mx_kscale(k):
    if not WIDE:
        return np.ones(k)
    levels = np.array([10, -10, 5, -5, 0])
    if k % 512:
        return np.exp2(np.random.permutation(np.resize(levels, k // 32))).repeat(32)
    a = np.empty((k // 512, 16))
    for p in range(k // 512):
        a[p, :8] = np.random.permutation(np.resize(levels, 8))
        for g in range(8):
            far = levels[np.abs(levels - a[p, g]) >= 10]
            a[p, g + 8] = far[np.random.randint(len(far))]
    return np.exp2(a.ravel()).repeat(32)


def f64(x):
    return np.asarray(x).astype(np.float64)


def striped(idx):
    return np.tile(idx.reshape(-1, 16).T, (8, 1)).astype(np.uint16)


def unstriped(offs):
    return offs[:16].T.reshape(-1).astype(np.int64)


def striped8(idx):
    return np.concatenate([x.reshape(-1, 16).T for x in idx]).astype(np.uint16)


def runs(offs, k):
    lists = np.stack([offs[16 * r : 16 * r + 16].T.reshape(-1) for r in range(8)]).astype(np.int64)
    return lists[np.arange(k) % 512 // 64]


def pack_weight(w):
    k, n = w.shape
    w = f64(np.asarray(w, np.float32).astype(ml_dtypes.bfloat16)).reshape(k // 32, 32, n)
    amax = np.abs(w).max(1)
    byte = np.clip(np.where(amax > 0, np.frexp(amax)[1] - 1 + 127 - 7, 1), 1, 254)
    scaled = (w * np.exp2(127.0 - byte)[:, None, :]).reshape(k, n).astype(np.float32)
    words = np.ascontiguousarray(scaled.reshape(k // 512, 128, 4, n).transpose(0, 1, 3, 2)).astype(ml_dtypes.float8_e4m3fn).view(np.uint8)
    return words, np.ascontiguousarray(byte.astype(np.uint8).reshape(k // 512, 16, n))


def unpack_weight(words, scales):
    g, p, n, _ = words.shape
    vals = np.ascontiguousarray(words).view(ml_dtypes.float8_e4m3fn).astype(np.float64) * np.repeat(np.exp2(scales.astype(np.float64) - 127.0), 8, axis=1)[..., None]
    return vals.transpose(0, 1, 3, 2).reshape(g * 512, n)


def silu(v):
    return v / (1.0 + np.exp(-np.maximum(v, -700.0)))

def planes(y):
    n, m = y.shape
    v = y.astype(np.float32).astype(ml_dtypes.bfloat16).astype(np.float64).reshape(n // 32, 32, m)
    top = np.abs(v).max(1)
    byte = np.clip(np.where(top > 0, np.frexp(top)[1] - 1 + 127 - 7, 1), 1, 254)
    codes = (v * np.exp2(127.0 - byte)[:, None, :]).reshape(n, m).astype(np.float32).astype(ml_dtypes.float8_e4m3fn).view(np.uint8)
    words = codes.reshape(n // 512, 128, 4, m).transpose(0, 1, 3, 2)
    return np.ascontiguousarray(words), np.ascontiguousarray(byte.astype(np.uint8).reshape(n // 512, 16, m))


K, T, S, V, N, H = 512, 2048, 512, 256, 512, 512


def setup_inputs():
    n = np.random.standard_normal
    s = mx_kscale(K)[:, None]
    u = mx_kscale(H)
    packed_xT = pack_weight(n((K, T)) * s)
    packed_w2 = pack_weight(n((H, N)) / np.sqrt(H) / u[:, None])
    return {
        "x_words": packed_xT[0],
        "x_scales": packed_xT[1],
        "w1": (n((K, H)) / np.sqrt(K) / s * u).astype(np.float32),
        "wt": np.repeat(np.random.uniform(0.3, 1.2, (8, V)), 64, axis=0).astype(np.float32),
        "w2_words": packed_w2[0],
        "w2_scales": packed_w2[1],
        "offs": striped(np.random.permutation(T)[:S]),
        "take": striped8(np.stack([np.random.permutation(S)[:V] for _ in range(8)])),
    }


def reference(x_words, x_scales, w1, wt, w2_words, w2_scales, offs, take):
    xq = unpack_weight(x_words, x_scales)[:, unstriped(offs)]
    y = mxq(f64(w1), 0, "e4m3").T @ xq
    e = (silu(y[np.arange(H)[:, None], runs(take, H)])) * f64(wt)
    d = np.zeros((H, S))
    d[np.arange(H)[:, None], runs(take, H)] = e
    z = y + d
    out_0 = unpack_weight(w2_words, w2_scales).T @ mxq(z, 0, "e4m3")
    return (out_0,) + planes(out_0)

@@ -1,0 +1,222 @@
+from contextlib import ExitStack
+
+import concourse.mybir as mybir
+
+K, T, S, V, H, N = 512, 2048, 512, 256, 512, 512
+FLOPS = 2 * K * H * S + 2 * H * N * S
+
+F32 = mybir.dt.float32
+BF16 = mybir.dt.bfloat16
+I32 = mybir.dt.int32
+U32 = mybir.dt.uint32
+U16 = mybir.dt.uint16
+U8 = mybir.dt.uint8
+FP8X4 = mybir.dt.float8_e4m3fn_x4
+SIGMOID = mybir.ActivationFunctionType.Sigmoid
+ADD = mybir.AluOpType.add
+MULT = mybir.AluOpType.mult
+
+P = 128
+PACK = 4
+QUADRANTS = 4
+QUADRANT = 32
+CHUNK = 128
+CHUNKS = S // CHUNK
+
+
+def tile_picked_headmod_silu_po_kernel(
+    tc, x_words, x_scales, w1, wt, w2_words, w2_scales, offs, take, out_0, out_1, out_2
+):
+    nc = tc.nc
+    with ExitStack() as ctx:
+        pool = ctx.enter_context(tc.tile_pool(name="sbuf", bufs=1))
+        psum = ctx.enter_context(tc.psum_pool(name="psum", bufs=1))
+
+        def sb(name, shape, dtype):
+            return pool.tile(shape, dtype, name=name, align_bytes=64)
+
+        def load_scale_rows(queue, plane, rows):
+            for q in range(QUADRANTS):
+                queue.dma_start(
+                    out=plane[QUADRANT * q : QUADRANT * q + PACK, :].bitcast(I32),
+                    in_=rows[PACK * q : PACK * q + PACK, :].bitcast(I32),
+                )
+
+        offs_sb = sb("offs_sb", [P, S // 16], U16)
+        take_sb = sb("take_sb", [P, V // 16], U16)
+        x_table = sb("x_table", [P, T], I32)
+        x_scale_table = sb("x_scale_table", [P, T], U8)
+        w1_raw = sb("w1_raw", [P, PACK, H], F32)
+        wt_sb = sb("wt_sb", [P, V], F32)
+        w2_table = sb("w2_table", [P, N], I32)
+        w2_scale_table = sb("w2_scale_table", [P, N], U8)
+        gates = [sb("gates%d" % t, [P, S], F32) for t in range(PACK)]
+        warm = sb("warm", [P, 8], F32)
+        warm_out = sb("warm_out", [P, 8], F32)
+
+        nc.vector.memset(x_scale_table[:].bitcast(I32), 0)
+        nc.vector.memset(warm[:], 0.0)
+        nc.scalar.activation(warm_out[:], warm[:], SIGMOID)
+        nc.vector.memset(w2_scale_table[:].bitcast(I32), 0)
+        for t in range(PACK):
+            nc.vector.memset(gates[t][:], 0.0)
+
+        nc.sync.dma_start(out=w1_raw[:], in_=w1.rearrange("(p j) c -> p j c", j=PACK))
+        nc.sync.dma_start(offs_sb[:], offs)
+        nc.sync.dma_start(out=x_table[:], in_=x_words[0].rearrange("p c r -> p (c r)").bitcast(I32))
+        load_scale_rows(nc.scalar, x_scale_table, x_scales[0])
+        nc.sync.dma_start(take_sb[:], take)
+        nc.sync.dma_start(out=wt_sb[:], in_=wt.rearrange("(p t) v -> p t v", t=PACK)[:, 0, :])
+        nc.sync.dma_start(out=w2_table[:], in_=w2_words[0].rearrange("p c r -> p (c r)").bitcast(I32))
+        load_scale_rows(nc.sync, w2_scale_table, w2_scales[0])
+
+        x_codes = sb("x_codes", [P, S], U32)
+        x_plane = sb("x_plane", [P, S], U8)
+        nc.vector.tensor_copy(x_plane[:], x_scale_table[:].indirect(offs_sb[:]))
+
+        w1_grouped = sb("w1_grouped", [P, H * PACK], BF16)
+        w1_view = w1_grouped[:].rearrange("p (t m j) -> p m j t", t=PACK, j=PACK)
+        w1_src = w1_raw[:].rearrange("p j (m t) -> p m j t", t=PACK)
+        split = 80
+        nc.vector.tensor_copy(w1_view[:, 0:split], w1_src[:, 0:split])
+        nc.scalar.copy(w1_view[:, split:P], w1_src[:, split:P])
+        w1_codes = sb("w1_codes", [P, H], U32)
+        w1_plane = sb("w1_plane", [P, H], U8)
+        nc.vector.quantize_mx(out=w1_codes[:].bitcast(FP8X4), scales=w1_plane[:], in_=w1_grouped[:])
+        for h in range(2):
+            nc.vector.tensor_copy(
+                x_codes[:, h * (S // 2) : (h + 1) * (S // 2)],
+                x_table[:].bitcast(U32).indirect(offs_sb[:, h * (S // 32) : (h + 1) * (S // 32)]),
+            )
+        y_sb = [sb("y%d" % t, [P, S], F32) for t in range(PACK)]
+        sig = [sb("sig%d" % t, [P, V], F32) for t in range(PACK)]
+
+        def first_product(t, cols, bank_name):
+            y_bank = psum.tile([P, S], F32, name=bank_name)
+            width = cols.stop - cols.start
+            nc.tensor.matmul_mx(
+                out=y_bank[:, 0:width],
+                lhsT=w1_codes[:, t * P : (t + 1) * P].bitcast(FP8X4),
+                lhsT_scale=w1_plane[:, t * P : (t + 1) * P],
+                rhs=x_codes[:, cols].bitcast(FP8X4),
+                rhs_scale=x_plane[:, cols],
+                start=True,
+                stop=True,
+            )
+            nc.scalar.copy(y_sb[t][:, cols], y_bank[:, 0:width])
+
+        def look_up(t, e0, e1):
+            nc.scalar.activation(sig[t][:, e0:e1], y_sb[t][:].indirect(take_sb[:, e0 // 16 : e1 // 16]), SIGMOID)
+
+        first_product(0, slice(0, S // 2), "bank0")
+        first_product(0, slice(S // 2, S), "bank1")
+        look_up(0, 0, V // 2)
+        look_up(0, V // 2, V)
+        for t in range(1, PACK):
+            first_product(t, slice(0, S), "bank1")
+            look_up(t, 0, V)
+
+        w2_codes = sb("w2_codes", [P, N], U32)
+        w2_plane = sb("w2_plane", [P, N], U8)
+        nc.vector.tensor_copy(
+            w2_codes[:].rearrange("p (t m) -> p m t", t=PACK),
+            w2_table[:].bitcast(U32).rearrange("p (m t) -> p m t", t=PACK),
+        )
+        nc.vector.tensor_copy(
+            w2_plane[:].rearrange("p (t m) -> p m t", t=PACK),
+            w2_scale_table[:].rearrange("p (m t) -> p m t", t=PACK),
+        )
+
+        z = sb("z", [P, CHUNKS, PACK, CHUNK], BF16)
+
+        def scatter(t, e0=0, e1=V):
+            nc.vector.tensor_tensor(
+                gates[t][:].indirect(take_sb[:, e0 // 16 : e1 // 16]), sig[t][:, e0:e1], wt_sb[:, e0:e1], MULT
+            )
+
+        def update(t, c0, c1):
+            cols = slice(c0 * CHUNK, c1 * CHUNK)
+            nc.vector.scalar_tensor_tensor(
+                out=z[:, c0:c1, t, :],
+                in0=gates[t][:, cols].rearrange("p (c n) -> p c n", n=CHUNK),
+                scalar=1.0,
+                in1=y_sb[t][:, cols].rearrange("p (c n) -> p c n", n=CHUNK),
+                op0=ADD,
+                op1=MULT,
+            )
+
+        scatter(0, 0, V // 2)
+        scatter(0, V // 2, V)
+        scatter(1)
+        update(0, 0, CHUNKS)
+        scatter(2)
+        update(1, 0, CHUNKS)
+        update(2, 0, CHUNKS)
+        scatter(3)
+
+        z_grouped = [sb("z_grouped%d" % c, [P, CHUNK * PACK], BF16) for c in range(CHUNKS)]
+        z_codes = [sb("z_codes%d" % c, [P, CHUNK], U32) for c in range(CHUNKS)]
+        z_plane = [sb("z_plane%d" % c, [P, CHUNK], U8) for c in range(CHUNKS)]
+        res = [sb("res%d" % c, [P, PACK, CHUNK], F32) for c in range(CHUNKS)]
+        res_grouped = [sb("res_grouped%d" % c, [P, CHUNK * PACK], BF16) for c in range(CHUNKS)]
+        res_codes = sb("res_codes", [P, S], U32)
+        res_plane = sb("res_plane", [P, S], U8)
+        out_rows = out_0.rearrange("(p t) s -> p t s", t=PACK)
+
+        def group(copy, dst, src):
+            copy(
+                dst.rearrange("p (n i t) -> p n t i", i=4, t=PACK),
+                src.rearrange("p t (n i) -> p n t i", i=4),
+            )
+
+        def group_z(c):
+            group(nc.scalar.copy if c % 2 == 1 else nc.vector.tensor_copy, z_grouped[c][:], z[:, c])
+
+        def second_product(c):
+            nc.vector.quantize_mx(out=z_codes[c][:].bitcast(FP8X4), scales=z_plane[c][:], in_=z_grouped[c][:])
+            bank = psum.tile([P, PACK, CHUNK], F32, name="bank%d" % (4 + c))
+            for t in range(PACK):
+                nc.tensor.matmul_mx(
+                    out=bank[:, t, :],
+                    lhsT=w2_codes[:, t * P : (t + 1) * P].bitcast(FP8X4),
+                    lhsT_scale=w2_plane[:, t * P : (t + 1) * P],
+                    rhs=z_codes[c][:].bitcast(FP8X4),
+                    rhs_scale=z_plane[c][:],
+                    start=True,
+                    stop=True,
+                )
+            nc.scalar.copy(res[c][:], bank[:])
+            nc.sync.dma_start(out=out_rows[:, :, c * CHUNK : (c + 1) * CHUNK], in_=res[c][:])
+
+        def quantize_result(c):
+            cols = slice(c * CHUNK, (c + 1) * CHUNK)
+            nc.vector.quantize_mx(out=res_codes[:, cols].bitcast(FP8X4), scales=res_plane[:, cols], in_=res_grouped[c][:])
+
+        update(3, 0, 1)
+        update(3, 1, 2)
+        group_z(0)
+        group_z(1)
+        second_product(0)
+        update(3, 2, 3)
+        second_product(1)
+        update(3, 3, 4)
+        group_z(2)
+        group_z(3)
+        second_product(2)
+        second_product(3)
+        group(nc.vector.tensor_copy, res_grouped[0][:], res[0][:])
+        for c in range(1, CHUNKS):
+            group(nc.vector.tensor_copy, res_grouped[c][:], res[c][:])
+            quantize_result(c - 1)
+        quantize_result(CHUNKS - 1)
+
+        out_words = out_1[0].rearrange("p c r -> p (c r)").bitcast(I32)
+        for h in range(2):
+            cols = slice(h * (S // 2), (h + 1) * (S // 2))
+            nc.sync.dma_start(out=out_words[:, cols], in_=res_codes[:, cols].bitcast(I32))
+        for q in range(QUADRANTS):
+            queue = nc.sync if q < 2 else nc.scalar
+            queue.dma_start(
+                out=out_2[0, PACK * q : PACK * q + PACK, :].bitcast(I32),
+                in_=res_plane[QUADRANT * q : QUADRANT * q + PACK, :].bitcast(I32),
+            )

@@ -30,6 +30,7 @@ def tile_picked_headmod_silu_po_kernel(
     nc = tc.nc
     with ExitStack() as ctx:
         pool = ctx.enter_context(tc.tile_pool(name="sbuf", bufs=1))
+        reuse = ctx.enter_context(tc.tile_pool(name="reuse", bufs=1))
         psum = ctx.enter_context(tc.psum_pool(name="psum", bufs=1))
 
         def sb(name, shape, dtype):
@@ -44,15 +45,17 @@ def tile_picked_headmod_silu_po_kernel(
 
         offs_sb = sb("offs_sb", [P, S // 16], U16)
         take_sb = sb("take_sb", [P, V // 16], U16)
-        x_table = sb("x_table", [P, T], I32)
+        X_AT = 4 * N
+        WT_AT = X_AT + 4 * T
+        warm = reuse.tile([P, 32], F32, name="warm", align_bytes=64, offset=X_AT - 64)
+        warm_out = reuse.tile([P, 32], F32, name="warm_out", align_bytes=64, offset=WT_AT)
+        x_table = reuse.tile([P, T], I32, name="x_table", align_bytes=64, offset=X_AT)
         x_scale_table = sb("x_scale_table", [P, T], U8)
         w1_raw = sb("w1_raw", [P, PACK, H], F32)
-        wt_sb = sb("wt_sb", [P, V], F32)
-        w2_table = sb("w2_table", [P, N], I32)
+        wt_sb = reuse.tile([P, V], F32, name="wt_sb", align_bytes=64, offset=WT_AT)
+        w2_table = reuse.tile([P, N], I32, name="w2_table", align_bytes=64, offset=0)
         w2_scale_table = sb("w2_scale_table", [P, N], U8)
         gates = [sb("gates%d" % t, [P, S], F32) for t in range(PACK)]
-        warm = sb("warm", [P, 8], F32)
-        warm_out = sb("warm_out", [P, 8], F32)
 
         nc.vector.memset(x_scale_table[:].bitcast(I32), 0)
         nc.vector.memset(warm[:], 0.0)
@@ -61,14 +64,14 @@ def tile_picked_headmod_silu_po_kernel(
         for t in range(PACK):
             nc.vector.memset(gates[t][:], 0.0)
 
-        nc.sync.dma_start(out=w1_raw[:], in_=w1.rearrange("(p j) c -> p j c", j=PACK))
         nc.sync.dma_start(offs_sb[:], offs)
-        nc.sync.dma_start(out=x_table[:], in_=x_words[0].rearrange("p c r -> p (c r)").bitcast(I32))
-        load_scale_rows(nc.scalar, x_scale_table, x_scales[0])
+        nc.sync.dma_start(out=w1_raw[:], in_=w1.rearrange("(p j) c -> p j c", j=PACK))
         nc.sync.dma_start(take_sb[:], take)
-        nc.sync.dma_start(out=wt_sb[:], in_=wt.rearrange("(p t) v -> p t v", t=PACK)[:, 0, :])
+        load_scale_rows(nc.sync, x_scale_table, x_scales[0])
+        nc.sync.dma_start(out=x_table[:], in_=x_words[0].rearrange("p c r -> p (c r)").bitcast(I32))
         nc.sync.dma_start(out=w2_table[:], in_=w2_words[0].rearrange("p c r -> p (c r)").bitcast(I32))
-        load_scale_rows(nc.sync, w2_scale_table, w2_scales[0])
+        nc.sync.dma_start(out=wt_sb[:], in_=wt.rearrange("(p t) v -> p t v", t=PACK)[:, 0, :])
+        load_scale_rows(nc.gpsimd, w2_scale_table, w2_scales[0])
 
         x_codes = sb("x_codes", [P, S], U32)
         x_plane = sb("x_plane", [P, S], U8)
@@ -88,11 +91,14 @@ def tile_picked_headmod_silu_po_kernel(
                 x_codes[:, h * (S // 2) : (h + 1) * (S // 2)],
                 x_table[:].bitcast(U32).indirect(offs_sb[:, h * (S // 32) : (h + 1) * (S // 32)]),
             )
-        y_sb = [sb("y%d" % t, [P, S], F32) for t in range(PACK)]
+        late = ctx.enter_context(tc.tile_pool(name="late", bufs=1))
+        y_sb = [late.tile([P, S], F32, name="y%d" % t, align_bytes=64, offset=(t + 2) % PACK * 4 * S * 2) for t in range(PACK)]
+        y_banks = {}
         sig = [sb("sig%d" % t, [P, V], F32) for t in range(PACK)]
 
-        def first_product(t, cols, bank_name):
+        def first_product(t, cols, bank_name, copy):
             y_bank = psum.tile([P, S], F32, name=bank_name)
+            y_banks[t] = y_bank
             width = cols.stop - cols.start
             nc.tensor.matmul_mx(
                 out=y_bank[:, 0:width],
@@ -103,21 +109,20 @@ def tile_picked_headmod_silu_po_kernel(
                 start=True,
                 stop=True,
             )
-            nc.scalar.copy(y_sb[t][:, cols], y_bank[:, 0:width])
+            copy(y_sb[t][:, cols], y_bank[:, 0:width])
 
         def look_up(t, e0, e1):
             nc.scalar.activation(sig[t][:, e0:e1], y_sb[t][:].indirect(take_sb[:, e0 // 16 : e1 // 16]), SIGMOID)
 
-        first_product(0, slice(0, S // 2), "bank0")
-        first_product(0, slice(S // 2, S), "bank1")
-        look_up(0, 0, V // 2)
-        look_up(0, V // 2, V)
+        first_product(0, slice(0, S // 2), "bank0", nc.scalar.copy)
+        first_product(0, slice(S // 2, S), "bank1", nc.scalar.copy)
+        look_up(0, 0, V)
         for t in range(1, PACK):
-            first_product(t, slice(0, S), "bank1")
+            first_product(t, slice(0, S), "bank%d" % (1 + t % 2), nc.vector.tensor_copy if t == 1 else nc.scalar.copy)
             look_up(t, 0, V)
 
-        w2_codes = sb("w2_codes", [P, N], U32)
-        w2_plane = sb("w2_plane", [P, N], U8)
+        w2_codes = reuse.tile([P, N], U32, name="w2_codes", align_bytes=64, offset=X_AT)
+        w2_plane = reuse.tile([P, N], U8, name="w2_plane", align_bytes=64, offset=X_AT + 4 * N)
         nc.vector.tensor_copy(
             w2_codes[:].rearrange("p (t m) -> p m t", t=PACK),
             w2_table[:].bitcast(U32).rearrange("p (m t) -> p m t", t=PACK),
@@ -127,7 +132,7 @@ def tile_picked_headmod_silu_po_kernel(
             w2_scale_table[:].rearrange("p (m t) -> p m t", t=PACK),
         )
 
-        z = sb("z", [P, CHUNKS, PACK, CHUNK], BF16)
+        z = late.tile([P, CHUNKS, PACK, CHUNK], BF16, name="z", align_bytes=64, offset=0)
 
         def scatter(t, e0=0, e1=V):
             nc.vector.tensor_tensor(
@@ -140,24 +145,25 @@ def tile_picked_headmod_silu_po_kernel(
                 out=z[:, c0:c1, t, :],
                 in0=gates[t][:, cols].rearrange("p (c n) -> p c n", n=CHUNK),
                 scalar=1.0,
-                in1=y_sb[t][:, cols].rearrange("p (c n) -> p c n", n=CHUNK),
+                in1=(y_banks[t] if t == 2 else y_sb[t])[:, cols].rearrange("p (c n) -> p c n", n=CHUNK),
                 op0=ADD,
                 op1=MULT,
             )
 
-        scatter(0, 0, V // 2)
-        scatter(0, V // 2, V)
+        scatter(0)
         scatter(1)
-        update(0, 0, CHUNKS)
         scatter(2)
+        update(0, 0, CHUNKS)
         update(1, 0, CHUNKS)
-        update(2, 0, CHUNKS)
         scatter(3)
+        update(2, 0, CHUNKS)
 
         z_grouped = [sb("z_grouped%d" % c, [P, CHUNK * PACK], BF16) for c in range(CHUNKS)]
         z_codes = [sb("z_codes%d" % c, [P, CHUNK], U32) for c in range(CHUNKS)]
         z_plane = [sb("z_plane%d" % c, [P, CHUNK], U8) for c in range(CHUNKS)]
-        res = [sb("res%d" % c, [P, PACK, CHUNK], F32) for c in range(CHUNKS)]
+        res_first = sb("res_first", [P, PACK, 2 * CHUNK], F32)
+        res_last = [sb("res%d" % c, [P, PACK, CHUNK], F32) for c in range(2, CHUNKS)]
+        res = [res_first[:, :, 0:CHUNK], res_first[:, :, CHUNK : 2 * CHUNK], res_last[0][:], res_last[1][:]]
         res_grouped = [sb("res_grouped%d" % c, [P, CHUNK * PACK], BF16) for c in range(CHUNKS)]
         res_codes = sb("res_codes", [P, S], U32)
         res_plane = sb("res_plane", [P, S], U8)
@@ -185,8 +191,11 @@ def tile_picked_headmod_silu_po_kernel(
                     start=True,
                     stop=True,
                 )
-            nc.scalar.copy(res[c][:], bank[:])
-            nc.sync.dma_start(out=out_rows[:, :, c * CHUNK : (c + 1) * CHUNK], in_=res[c][:])
+            nc.scalar.copy(res[c], bank[:])
+            if c == 1:
+                nc.sync.dma_start(out=out_rows[:, :, 0 : 2 * CHUNK], in_=res_first[:])
+            elif c > 1:
+                nc.sync.dma_start(out=out_rows[:, :, c * CHUNK : (c + 1) * CHUNK], in_=res[c])
 
         def quantize_result(c):
             cols = slice(c * CHUNK, (c + 1) * CHUNK)
@@ -204,9 +213,9 @@ def tile_picked_headmod_silu_po_kernel(
         group_z(3)
         second_product(2)
         second_product(3)
-        group(nc.vector.tensor_copy, res_grouped[0][:], res[0][:])
+        group(nc.vector.tensor_copy, res_grouped[0][:], res[0])
         for c in range(1, CHUNKS):
-            group(nc.vector.tensor_copy, res_grouped[c][:], res[c][:])
+            group(nc.vector.tensor_copy, res_grouped[c][:], res[c])
             quantize_result(c - 1)
         quantize_result(CHUNKS - 1)
 

@@ -48,13 +48,13 @@ def tile_picked_headmod_silu_po_kernel(
         X_AT = 4 * N
         WT_AT = X_AT + 4 * T
         warm = reuse.tile([P, 32], F32, name="warm", align_bytes=64, offset=X_AT - 64)
-        warm_out = reuse.tile([P, 32], F32, name="warm_out", align_bytes=64, offset=WT_AT)
+        warm_out = reuse.tile([P, 32], F32, name="warm_out", align_bytes=64, offset=WT_AT + 4 * V - 64)
         x_table = reuse.tile([P, T], I32, name="x_table", align_bytes=64, offset=X_AT)
         x_scale_table = sb("x_scale_table", [P, T], U8)
         w1_raw = sb("w1_raw", [P, PACK, H], F32)
         wt_sb = reuse.tile([P, V], F32, name="wt_sb", align_bytes=64, offset=WT_AT)
         w2_table = reuse.tile([P, N], I32, name="w2_table", align_bytes=64, offset=0)
-        w2_scale_table = sb("w2_scale_table", [P, N], U8)
+        w2_scale_table = reuse.tile([P, N], U8, name="w2_scale_table", align_bytes=64, offset=WT_AT + 4 * V)
         gates = [sb("gates%d" % t, [P, S], F32) for t in range(PACK)]
 
         nc.vector.memset(x_scale_table[:].bitcast(I32), 0)
@@ -71,7 +71,7 @@ def tile_picked_headmod_silu_po_kernel(
         nc.sync.dma_start(out=x_table[:], in_=x_words[0].rearrange("p c r -> p (c r)").bitcast(I32))
         nc.sync.dma_start(out=w2_table[:], in_=w2_words[0].rearrange("p c r -> p (c r)").bitcast(I32))
         nc.sync.dma_start(out=wt_sb[:], in_=wt.rearrange("(p t) v -> p t v", t=PACK)[:, 0, :])
-        load_scale_rows(nc.gpsimd, w2_scale_table, w2_scales[0])
+        load_scale_rows(nc.sync, w2_scale_table, w2_scales[0])
 
         x_codes = sb("x_codes", [P, S], U32)
         x_plane = sb("x_plane", [P, S], U8)
@@ -80,16 +80,28 @@ def tile_picked_headmod_silu_po_kernel(
         w1_grouped = sb("w1_grouped", [P, H * PACK], BF16)
         w1_view = w1_grouped[:].rearrange("p (t m j) -> p m j t", t=PACK, j=PACK)
         w1_src = w1_raw[:].rearrange("p j (m t) -> p m j t", t=PACK)
-        split = 80
+        split = 72
         nc.vector.tensor_copy(w1_view[:, 0:split], w1_src[:, 0:split])
         nc.scalar.copy(w1_view[:, split:P], w1_src[:, split:P])
-        w1_codes = sb("w1_codes", [P, H], U32)
-        w1_plane = sb("w1_plane", [P, H], U8)
-        nc.vector.quantize_mx(out=w1_codes[:].bitcast(FP8X4), scales=w1_plane[:], in_=w1_grouped[:])
+        REST_AT = X_AT + 8 * N
+        first_codes = sb("first_codes", [P, P], U32)
+        first_plane = sb("first_plane", [P, P], U8)
+        rest_codes = reuse.tile([P, H - P], U32, name="rest_codes", align_bytes=64, offset=REST_AT)
+        rest_plane = sb("rest_plane", [P, H - P], U8)
+        w1_codes = [first_codes[:]] + [rest_codes[:, t * P : (t + 1) * P] for t in range(PACK - 1)]
+        w1_plane = [first_plane[:]] + [rest_plane[:, t * P : (t + 1) * P] for t in range(PACK - 1)]
+        nc.vector.quantize_mx(out=first_codes[:].bitcast(FP8X4), scales=first_plane[:], in_=w1_grouped[:, 0 : P * PACK])
         for h in range(2):
             nc.vector.tensor_copy(
                 x_codes[:, h * (S // 2) : (h + 1) * (S // 2)],
                 x_table[:].bitcast(U32).indirect(offs_sb[:, h * (S // 32) : (h + 1) * (S // 32)]),
+            )
+        for t0, t1 in ((1, 2), (2, 4)):
+            cols = slice((t0 - 1) * P, (t1 - 1) * P)
+            nc.vector.quantize_mx(
+                out=rest_codes[:, cols].bitcast(FP8X4),
+                scales=rest_plane[:, cols],
+                in_=w1_grouped[:, t0 * P * PACK : t1 * P * PACK],
             )
         late = ctx.enter_context(tc.tile_pool(name="late", bufs=1))
         y_sb = [late.tile([P, S], F32, name="y%d" % t, align_bytes=64, offset=(t + 2) % PACK * 4 * S * 2) for t in range(PACK)]
@@ -102,8 +114,8 @@ def tile_picked_headmod_silu_po_kernel(
             width = cols.stop - cols.start
             nc.tensor.matmul_mx(
                 out=y_bank[:, 0:width],
-                lhsT=w1_codes[:, t * P : (t + 1) * P].bitcast(FP8X4),
-                lhsT_scale=w1_plane[:, t * P : (t + 1) * P],
+                lhsT=w1_codes[t].bitcast(FP8X4),
+                lhsT_scale=w1_plane[t],
                 rhs=x_codes[:, cols].bitcast(FP8X4),
                 rhs_scale=x_plane[:, cols],
                 start=True,
@@ -128,8 +140,8 @@ def tile_picked_headmod_silu_po_kernel(
             w2_table[:].bitcast(U32).rearrange("p (m t) -> p m t", t=PACK),
         )
         nc.vector.tensor_copy(
-            w2_plane[:].rearrange("p (t m) -> p m t", t=PACK),
-            w2_scale_table[:].rearrange("p (m t) -> p m t", t=PACK),
+            w2_plane[:].rearrange("p (t m) -> p t m", t=PACK),
+            w2_scale_table[:].rearrange("p (m t) -> p t m", t=PACK),
         )
 
         z = late.tile([P, CHUNKS, PACK, CHUNK], BF16, name="z", align_bytes=64, offset=0)
@@ -164,7 +176,8 @@ def tile_picked_headmod_silu_po_kernel(
         res_first = sb("res_first", [P, PACK, 2 * CHUNK], F32)
         res_last = [sb("res%d" % c, [P, PACK, CHUNK], F32) for c in range(2, CHUNKS)]
         res = [res_first[:, :, 0:CHUNK], res_first[:, :, CHUNK : 2 * CHUNK], res_last[0][:], res_last[1][:]]
-        res_grouped = [sb("res_grouped%d" % c, [P, CHUNK * PACK], BF16) for c in range(CHUNKS)]
+        pieces = ((0, 2, res_first), (2, 3, res_last[0]), (3, 4, res_last[1]))
+        res_grouped = [sb("res_grouped%d" % c0, [P, (c1 - c0) * CHUNK * PACK], BF16) for c0, c1, src in pieces]
         res_codes = sb("res_codes", [P, S], U32)
         res_plane = sb("res_plane", [P, S], U8)
         out_rows = out_0.rearrange("(p t) s -> p t s", t=PACK)
@@ -180,26 +193,28 @@ def tile_picked_headmod_silu_po_kernel(
 
         def second_product(c):
             nc.vector.quantize_mx(out=z_codes[c][:].bitcast(FP8X4), scales=z_plane[c][:], in_=z_grouped[c][:])
-            bank = psum.tile([P, PACK, CHUNK], F32, name="bank%d" % (4 + c))
-            for t in range(PACK):
-                nc.tensor.matmul_mx(
-                    out=bank[:, t, :],
-                    lhsT=w2_codes[:, t * P : (t + 1) * P].bitcast(FP8X4),
-                    lhsT_scale=w2_plane[:, t * P : (t + 1) * P],
-                    rhs=z_codes[c][:].bitcast(FP8X4),
-                    rhs_scale=z_plane[c][:],
-                    start=True,
-                    stop=True,
-                )
-            nc.scalar.copy(res[c], bank[:])
+            parts = ((0, PACK, 4 + c),) if c < CHUNKS - 1 else ((0, 2, 7), (2, PACK, 3))
+            for t0, t1, number in parts:
+                bank = psum.tile([P, PACK, CHUNK], F32, name="bank%d" % number)
+                for t in range(t0, t1):
+                    nc.tensor.matmul_mx(
+                        out=bank[:, t, :],
+                        lhsT=w2_codes[:, t * P : (t + 1) * P].bitcast(FP8X4),
+                        lhsT_scale=w2_plane[:, t * P : (t + 1) * P],
+                        rhs=z_codes[c][:].bitcast(FP8X4),
+                        rhs_scale=z_plane[c][:],
+                        start=True,
+                        stop=True,
+                    )
+                nc.scalar.copy(res[c][:, t0:t1, :], bank[:, t0:t1, :])
             if c == 1:
                 nc.sync.dma_start(out=out_rows[:, :, 0 : 2 * CHUNK], in_=res_first[:])
             elif c > 1:
                 nc.sync.dma_start(out=out_rows[:, :, c * CHUNK : (c + 1) * CHUNK], in_=res[c])
 
-        def quantize_result(c):
-            cols = slice(c * CHUNK, (c + 1) * CHUNK)
-            nc.vector.quantize_mx(out=res_codes[:, cols].bitcast(FP8X4), scales=res_plane[:, cols], in_=res_grouped[c][:])
+        def quantize_result(i):
+            cols = slice(pieces[i][0] * CHUNK, pieces[i][1] * CHUNK)
+            nc.vector.quantize_mx(out=res_codes[:, cols].bitcast(FP8X4), scales=res_plane[:, cols], in_=res_grouped[i][:])
 
         update(3, 0, 1)
         update(3, 1, 2)
@@ -213,15 +228,14 @@ def tile_picked_headmod_silu_po_kernel(
         group_z(3)
         second_product(2)
         second_product(3)
-        group(nc.vector.tensor_copy, res_grouped[0][:], res[0])
-        for c in range(1, CHUNKS):
-            group(nc.vector.tensor_copy, res_grouped[c][:], res[c])
-            quantize_result(c - 1)
-        quantize_result(CHUNKS - 1)
+        group(nc.vector.tensor_copy, res_grouped[0][:], res_first[:])
+        for i in range(1, len(pieces)):
+            group(nc.vector.tensor_copy, res_grouped[i][:], pieces[i][2][:])
+            quantize_result(i - 1)
+        quantize_result(len(pieces) - 1)
 
         out_words = out_1[0].rearrange("p c r -> p (c r)").bitcast(I32)
-        for h in range(2):
-            cols = slice(h * (S // 2), (h + 1) * (S // 2))
+        for cols in (slice(0, 3 * CHUNK), slice(3 * CHUNK, S)):
             nc.sync.dma_start(out=out_words[:, cols], in_=res_codes[:, cols].bitcast(I32))
         for q in range(QUADRANTS):
             queue = nc.sync if q < 2 else nc.scalar

@@ -168,15 +168,15 @@ def tile_picked_headmod_silu_po_kernel(
         update(0, 0, CHUNKS)
         update(1, 0, CHUNKS)
         scatter(3)
-        update(2, 0, CHUNKS)
+        update(2, 0, 1)
 
         z_grouped = [sb("z_grouped%d" % c, [P, CHUNK * PACK], BF16) for c in range(CHUNKS)]
         z_codes = [sb("z_codes%d" % c, [P, CHUNK], U32) for c in range(CHUNKS)]
         z_plane = [sb("z_plane%d" % c, [P, CHUNK], U8) for c in range(CHUNKS)]
         res_first = sb("res_first", [P, PACK, 2 * CHUNK], F32)
-        res_last = [sb("res%d" % c, [P, PACK, CHUNK], F32) for c in range(2, CHUNKS)]
-        res = [res_first[:, :, 0:CHUNK], res_first[:, :, CHUNK : 2 * CHUNK], res_last[0][:], res_last[1][:]]
-        pieces = ((0, 2, res_first), (2, 3, res_last[0]), (3, 4, res_last[1]))
+        res_last = sb("res_last", [P, PACK, 2 * CHUNK], F32)
+        res = [pair[:, :, h * CHUNK : (h + 1) * CHUNK] for pair in (res_first, res_last) for h in range(2)]
+        pieces = ((0, 2, res_first[:]), (2, 3, res[2]), (3, 4, res[3]))
         res_grouped = [sb("res_grouped%d" % c0, [P, (c1 - c0) * CHUNK * PACK], BF16) for c0, c1, src in pieces]
         res_codes = sb("res_codes", [P, S], U32)
         res_plane = sb("res_plane", [P, S], U8)
@@ -193,7 +193,7 @@ def tile_picked_headmod_silu_po_kernel(
 
         def second_product(c):
             nc.vector.quantize_mx(out=z_codes[c][:].bitcast(FP8X4), scales=z_plane[c][:], in_=z_grouped[c][:])
-            parts = ((0, PACK, 4 + c),) if c < CHUNKS - 1 else ((0, 2, 7), (2, PACK, 3))
+            parts = ((0, PACK, 4 + c),) if c > 0 else ((0, 2, 3), (2, PACK, 4))
             for t0, t1, number in parts:
                 bank = psum.tile([P, PACK, CHUNK], F32, name="bank%d" % number)
                 for t in range(t0, t1):
@@ -207,18 +207,19 @@ def tile_picked_headmod_silu_po_kernel(
                         stop=True,
                     )
                 nc.scalar.copy(res[c][:, t0:t1, :], bank[:, t0:t1, :])
-            if c == 1:
-                nc.sync.dma_start(out=out_rows[:, :, 0 : 2 * CHUNK], in_=res_first[:])
-            elif c > 1:
-                nc.sync.dma_start(out=out_rows[:, :, c * CHUNK : (c + 1) * CHUNK], in_=res[c])
+                if c < 2:
+                    nc.sync.dma_start(out=out_rows[:, t0:t1, c * CHUNK : (c + 1) * CHUNK], in_=res[c][:, t0:t1, :])
+            if c == CHUNKS - 1:
+                nc.sync.dma_start(out=out_rows[:, :, 2 * CHUNK : S], in_=res_last[:])
 
         def quantize_result(i):
             cols = slice(pieces[i][0] * CHUNK, pieces[i][1] * CHUNK)
             nc.vector.quantize_mx(out=res_codes[:, cols].bitcast(FP8X4), scales=res_plane[:, cols], in_=res_grouped[i][:])
 
         update(3, 0, 1)
-        update(3, 1, 2)
+        update(2, 1, CHUNKS)
         group_z(0)
+        update(3, 1, 2)
         group_z(1)
         second_product(0)
         update(3, 2, 3)
@@ -230,7 +231,7 @@ def tile_picked_headmod_silu_po_kernel(
         second_product(3)
         group(nc.vector.tensor_copy, res_grouped[0][:], res_first[:])
         for i in range(1, len(pieces)):
-            group(nc.vector.tensor_copy, res_grouped[i][:], pieces[i][2][:])
+            group(nc.vector.tensor_copy, res_grouped[i][:], pieces[i][2])
             quantize_result(i - 1)
         quantize_result(len(pieces) - 1)
 
@@ -238,8 +239,7 @@ def tile_picked_headmod_silu_po_kernel(
         for cols in (slice(0, 3 * CHUNK), slice(3 * CHUNK, S)):
             nc.sync.dma_start(out=out_words[:, cols], in_=res_codes[:, cols].bitcast(I32))
         for q in range(QUADRANTS):
-            queue = nc.sync if q < 2 else nc.scalar
-            queue.dma_start(
+            nc.scalar.dma_start(
                 out=out_2[0, PACK * q : PACK * q + PACK, :].bitcast(I32),
                 in_=res_plane[QUADRANT * q : QUADRANT * q + PACK, :].bitcast(I32),
             )

@@ -36,72 +36,76 @@ def tile_picked_headmod_silu_po_kernel(
         def sb(name, shape, dtype):
             return pool.tile(shape, dtype, name=name, align_bytes=64)
 
-        def load_scale_rows(queue, plane, rows):
+        def move_scale_rows(plane, rows):
             for q in range(QUADRANTS):
-                queue.dma_start(
+                nc.sync.dma_start(
                     out=plane[QUADRANT * q : QUADRANT * q + PACK, :].bitcast(I32),
                     in_=rows[PACK * q : PACK * q + PACK, :].bitcast(I32),
                 )
 
         offs_sb = sb("offs_sb", [P, S // 16], U16)
         take_sb = sb("take_sb", [P, V // 16], U16)
-        X_AT = 4 * N
-        WT_AT = X_AT + 4 * T
-        warm = reuse.tile([P, 32], F32, name="warm", align_bytes=64, offset=X_AT - 64)
-        warm_out = reuse.tile([P, 32], F32, name="warm_out", align_bytes=64, offset=WT_AT + 4 * V - 64)
-        x_table = reuse.tile([P, T], I32, name="x_table", align_bytes=64, offset=X_AT)
-        x_scale_table = sb("x_scale_table", [P, T], U8)
+        ROWS = 16
+        WT_AT = 4 * N
+        warm = sb("warm", [P, 32], F32)
+        warm_out = sb("warm_out", [P, 32], F32)
+        x_table = sb("x_table", [P, T], I32)
+        x_scale_table = reuse.tile([P, T], U8, name="x_scale_table", align_bytes=64, offset=WT_AT - T // 2)
         w1_raw = sb("w1_raw", [P, PACK, H], F32)
         wt_sb = reuse.tile([P, V], F32, name="wt_sb", align_bytes=64, offset=WT_AT)
         w2_table = reuse.tile([P, N], I32, name="w2_table", align_bytes=64, offset=0)
-        w2_scale_table = reuse.tile([P, N], U8, name="w2_scale_table", align_bytes=64, offset=WT_AT + 4 * V)
+        w2_scale_table = sb("w2_scale_table", [P, N], U8)
         gates = [sb("gates%d" % t, [P, S], F32) for t in range(PACK)]
+        x_plane = sb("x_plane", [P, S], U8)
+        w2_plane = sb("w2_plane", [P, N], U8)
 
         nc.vector.memset(x_scale_table[:].bitcast(I32), 0)
+        nc.vector.memset(w2_scale_table[:].bitcast(I32), 0)
         nc.vector.memset(warm[:], 0.0)
         nc.scalar.activation(warm_out[:], warm[:], SIGMOID)
-        nc.vector.memset(w2_scale_table[:].bitcast(I32), 0)
+        nc.vector.memset(x_plane[:].bitcast(I32), 0)
+        nc.vector.memset(w2_plane[:].bitcast(I32), 0)
         for t in range(PACK):
             nc.vector.memset(gates[t][:], 0.0)
 
+        w1_rows = w1.rearrange("(p j) c -> p j c", j=PACK)
         nc.sync.dma_start(offs_sb[:], offs)
-        nc.sync.dma_start(out=w1_raw[:], in_=w1.rearrange("(p j) c -> p j c", j=PACK))
-        nc.sync.dma_start(take_sb[:], take)
-        load_scale_rows(nc.sync, x_scale_table, x_scales[0])
+        nc.sync.dma_start(out=w1_raw[:, 0:2], in_=w1_rows[:, 0:2])
+        nc.sync.dma_start(out=x_scale_table[0:ROWS, :].bitcast(I32), in_=x_scales[0].bitcast(I32))
+        nc.sync.dma_start(out=w2_scale_table[0:ROWS, :].bitcast(I32), in_=w2_scales[0].bitcast(I32))
+        nc.sync.dma_start(out=w1_raw[:, 2:4], in_=w1_rows[:, 2:4])
         nc.sync.dma_start(out=x_table[:], in_=x_words[0].rearrange("p c r -> p (c r)").bitcast(I32))
+        nc.sync.dma_start(take_sb[:], take)
+
+        GROUPED_AT = WT_AT + 4 * V
+        x_rows = sb("x_rows", [P, S], U8)
+        nc.vector.tensor_copy(x_rows[:], x_scale_table[:].indirect(offs_sb[:]))
+        move_scale_rows(x_plane, x_rows)
         nc.sync.dma_start(out=w2_table[:], in_=w2_words[0].rearrange("p c r -> p (c r)").bitcast(I32))
         nc.sync.dma_start(out=wt_sb[:], in_=wt.rearrange("(p t) v -> p t v", t=PACK)[:, 0, :])
-        load_scale_rows(nc.sync, w2_scale_table, w2_scales[0])
+        w2_rows = sb("w2_rows", [P, N], U8)
+        nc.vector.tensor_copy(
+            w2_rows[:].rearrange("p (t m) -> p t m", t=PACK),
+            w2_scale_table[:].rearrange("p (m t) -> p t m", t=PACK),
+        )
+        move_scale_rows(w2_plane, w2_rows)
 
-        x_codes = sb("x_codes", [P, S], U32)
-        x_plane = sb("x_plane", [P, S], U8)
-        nc.vector.tensor_copy(x_plane[:], x_scale_table[:].indirect(offs_sb[:]))
-
-        w1_grouped = sb("w1_grouped", [P, H * PACK], BF16)
+        w1_grouped = reuse.tile([P, H * PACK], BF16, name="w1_grouped", align_bytes=64, offset=GROUPED_AT)
         w1_view = w1_grouped[:].rearrange("p (t m j) -> p m j t", t=PACK, j=PACK)
         w1_src = w1_raw[:].rearrange("p j (m t) -> p m j t", t=PACK)
-        split = 72
+        split = 80
         nc.vector.tensor_copy(w1_view[:, 0:split], w1_src[:, 0:split])
         nc.scalar.copy(w1_view[:, split:P], w1_src[:, split:P])
-        REST_AT = X_AT + 8 * N
-        first_codes = sb("first_codes", [P, P], U32)
-        first_plane = sb("first_plane", [P, P], U8)
-        rest_codes = reuse.tile([P, H - P], U32, name="rest_codes", align_bytes=64, offset=REST_AT)
-        rest_plane = sb("rest_plane", [P, H - P], U8)
-        w1_codes = [first_codes[:]] + [rest_codes[:, t * P : (t + 1) * P] for t in range(PACK - 1)]
-        w1_plane = [first_plane[:]] + [rest_plane[:, t * P : (t + 1) * P] for t in range(PACK - 1)]
-        nc.vector.quantize_mx(out=first_codes[:].bitcast(FP8X4), scales=first_plane[:], in_=w1_grouped[:, 0 : P * PACK])
+        w1_codes_all = sb("w1_codes_all", [P, H], U32)
+        w1_plane_all = sb("w1_plane_all", [P, H], U8)
+        w1_codes = [w1_codes_all[:, t * P : (t + 1) * P] for t in range(PACK)]
+        w1_plane = [w1_plane_all[:, t * P : (t + 1) * P] for t in range(PACK)]
+        nc.vector.quantize_mx(out=w1_codes_all[:].bitcast(FP8X4), scales=w1_plane_all[:], in_=w1_grouped[:])
+        x_codes = reuse.tile([P, S], U32, name="x_codes", align_bytes=64, offset=GROUPED_AT)
         for h in range(2):
             nc.vector.tensor_copy(
                 x_codes[:, h * (S // 2) : (h + 1) * (S // 2)],
                 x_table[:].bitcast(U32).indirect(offs_sb[:, h * (S // 32) : (h + 1) * (S // 32)]),
-            )
-        for t0, t1 in ((1, 2), (2, 4)):
-            cols = slice((t0 - 1) * P, (t1 - 1) * P)
-            nc.vector.quantize_mx(
-                out=rest_codes[:, cols].bitcast(FP8X4),
-                scales=rest_plane[:, cols],
-                in_=w1_grouped[:, t0 * P * PACK : t1 * P * PACK],
             )
         late = ctx.enter_context(tc.tile_pool(name="late", bufs=1))
         y_sb = [late.tile([P, S], F32, name="y%d" % t, align_bytes=64, offset=(t + 2) % PACK * 4 * S * 2) for t in range(PACK)]
@@ -133,15 +137,10 @@ def tile_picked_headmod_silu_po_kernel(
             first_product(t, slice(0, S), "bank%d" % (1 + t % 2), nc.vector.tensor_copy if t == 1 else nc.scalar.copy)
             look_up(t, 0, V)
 
-        w2_codes = reuse.tile([P, N], U32, name="w2_codes", align_bytes=64, offset=X_AT)
-        w2_plane = reuse.tile([P, N], U8, name="w2_plane", align_bytes=64, offset=X_AT + 4 * N)
+        w2_codes = sb("w2_codes", [P, N], U32)
         nc.vector.tensor_copy(
             w2_codes[:].rearrange("p (t m) -> p m t", t=PACK),
             w2_table[:].bitcast(U32).rearrange("p (m t) -> p m t", t=PACK),
-        )
-        nc.vector.tensor_copy(
-            w2_plane[:].rearrange("p (t m) -> p t m", t=PACK),
-            w2_scale_table[:].rearrange("p (m t) -> p t m", t=PACK),
         )
 
         z = late.tile([P, CHUNKS, PACK, CHUNK], BF16, name="z", align_bytes=64, offset=0)

@@ -91,11 +91,11 @@ def tile_picked_headmod_silu_po_kernel(
         move_scale_rows(w2_plane, w2_rows)
 
         w1_grouped = reuse.tile([P, H * PACK], BF16, name="w1_grouped", align_bytes=64, offset=GROUPED_AT)
-        w1_view = w1_grouped[:].rearrange("p (t m j) -> p m j t", t=PACK, j=PACK)
-        w1_src = w1_raw[:].rearrange("p j (m t) -> p m j t", t=PACK)
+        w1_view = w1_grouped[:].rearrange("p (u e m j) -> p u m j e", u=2, e=2, j=PACK)
+        w1_src = w1_raw[:].rearrange("p j (m u e) -> p u m j e", u=2, e=2)
         split = 80
-        nc.vector.tensor_copy(w1_view[:, 0:split], w1_src[:, 0:split])
-        nc.scalar.copy(w1_view[:, split:P], w1_src[:, split:P])
+        nc.vector.tensor_copy(w1_view[:, :, 0:split], w1_src[:, :, 0:split])
+        nc.scalar.copy(w1_view[:, :, split:P], w1_src[:, :, split:P])
         w1_codes_all = sb("w1_codes_all", [P, H], U32)
         w1_plane_all = sb("w1_plane_all", [P, H], U8)
         w1_codes = [w1_codes_all[:, t * P : (t + 1) * P] for t in range(PACK)]

@@ -46,11 +46,12 @@ def tile_picked_headmod_silu_po_kernel(
         offs_sb = sb("offs_sb", [P, S // 16], U16)
         take_sb = sb("take_sb", [P, V // 16], U16)
         ROWS = 16
-        WT_AT = 4 * N
+        W2_ROWS_AT = 4 * N
+        WT_AT = W2_ROWS_AT + 2 * N
         warm = sb("warm", [P, 32], F32)
         warm_out = sb("warm_out", [P, 32], F32)
         x_table = sb("x_table", [P, T], I32)
-        x_scale_table = reuse.tile([P, T], U8, name="x_scale_table", align_bytes=64, offset=WT_AT - T // 2)
+        x_scale_table = reuse.tile([P, T], U8, name="x_scale_table", align_bytes=64, offset=W2_ROWS_AT - N)
         w1_raw = sb("w1_raw", [P, PACK, H], F32)
         wt_sb = reuse.tile([P, V], F32, name="wt_sb", align_bytes=64, offset=WT_AT)
         w2_table = reuse.tile([P, N], I32, name="w2_table", align_bytes=64, offset=0)
@@ -68,44 +69,45 @@ def tile_picked_headmod_silu_po_kernel(
         for t in range(PACK):
             nc.vector.memset(gates[t][:], 0.0)
 
-        w1_rows = w1.rearrange("(p j) c -> p j c", j=PACK)
+        x_rows_hbm = x_words[0].rearrange("p c r -> p (c r)").bitcast(I32)
         nc.sync.dma_start(offs_sb[:], offs)
-        nc.sync.dma_start(out=w1_raw[:, 0:2], in_=w1_rows[:, 0:2])
+        nc.sync.dma_start(out=x_table[:, 0 : T // 2], in_=x_rows_hbm[:, 0 : T // 2])
         nc.sync.dma_start(out=x_scale_table[0:ROWS, :].bitcast(I32), in_=x_scales[0].bitcast(I32))
         nc.sync.dma_start(out=w2_scale_table[0:ROWS, :].bitcast(I32), in_=w2_scales[0].bitcast(I32))
-        nc.sync.dma_start(out=w1_raw[:, 2:4], in_=w1_rows[:, 2:4])
-        nc.sync.dma_start(out=x_table[:], in_=x_words[0].rearrange("p c r -> p (c r)").bitcast(I32))
+        nc.sync.dma_start(out=x_table[:, T // 2 : T], in_=x_rows_hbm[:, T // 2 : T])
+        nc.sync.dma_start(out=w1_raw[:], in_=w1.rearrange("(p j) c -> p j c", j=PACK))
         nc.sync.dma_start(take_sb[:], take)
 
-        GROUPED_AT = WT_AT + 4 * V
         x_rows = sb("x_rows", [P, S], U8)
         nc.vector.tensor_copy(x_rows[:], x_scale_table[:].indirect(offs_sb[:]))
         move_scale_rows(x_plane, x_rows)
         nc.sync.dma_start(out=w2_table[:], in_=w2_words[0].rearrange("p c r -> p (c r)").bitcast(I32))
         nc.sync.dma_start(out=wt_sb[:], in_=wt.rearrange("(p t) v -> p t v", t=PACK)[:, 0, :])
-        w2_rows = sb("w2_rows", [P, N], U8)
+        w2_rows = reuse.tile([P, N], U8, name="w2_rows", align_bytes=64, offset=W2_ROWS_AT)
         nc.vector.tensor_copy(
             w2_rows[:].rearrange("p (t m) -> p t m", t=PACK),
             w2_scale_table[:].rearrange("p (m t) -> p t m", t=PACK),
         )
         move_scale_rows(w2_plane, w2_rows)
 
-        w1_grouped = reuse.tile([P, H * PACK], BF16, name="w1_grouped", align_bytes=64, offset=GROUPED_AT)
-        w1_view = w1_grouped[:].rearrange("p (u e m j) -> p u m j e", u=2, e=2, j=PACK)
+        x_codes = sb("x_codes", [P, S], U32)
+        nc.vector.tensor_copy(x_codes[:], x_table[:].bitcast(U32).indirect(offs_sb[:]))
+
+        w1_grouped = [sb("w1_grouped%d" % u, [P, H * 2], BF16) for u in range(2)]
         w1_src = w1_raw[:].rearrange("p j (m u e) -> p u m j e", u=2, e=2)
-        split = 80
-        nc.vector.tensor_copy(w1_view[:, :, 0:split], w1_src[:, :, 0:split])
-        nc.scalar.copy(w1_view[:, :, split:P], w1_src[:, :, split:P])
         w1_codes_all = sb("w1_codes_all", [P, H], U32)
         w1_plane_all = sb("w1_plane_all", [P, H], U8)
         w1_codes = [w1_codes_all[:, t * P : (t + 1) * P] for t in range(PACK)]
         w1_plane = [w1_plane_all[:, t * P : (t + 1) * P] for t in range(PACK)]
-        nc.vector.quantize_mx(out=w1_codes_all[:].bitcast(FP8X4), scales=w1_plane_all[:], in_=w1_grouped[:])
-        x_codes = reuse.tile([P, S], U32, name="x_codes", align_bytes=64, offset=GROUPED_AT)
-        for h in range(2):
-            nc.vector.tensor_copy(
-                x_codes[:, h * (S // 2) : (h + 1) * (S // 2)],
-                x_table[:].bitcast(U32).indirect(offs_sb[:, h * (S // 32) : (h + 1) * (S // 32)]),
+        for u, split in ((0, 88), (1, 40)):
+            view = w1_grouped[u][:].rearrange("p (e m j) -> p m j e", e=2, j=PACK)
+            nc.vector.tensor_copy(view[:, 0:split], w1_src[:, u, 0:split])
+            nc.scalar.copy(view[:, split:P], w1_src[:, u, split:P])
+        for t0, t1 in ((0, 1), (1, 2), (2, 4)):
+            nc.vector.quantize_mx(
+                out=w1_codes_all[:, t0 * P : t1 * P].bitcast(FP8X4),
+                scales=w1_plane_all[:, t0 * P : t1 * P],
+                in_=w1_grouped[t0 // 2][:, (t0 % 2) * P * PACK : (t0 % 2 + t1 - t0) * P * PACK],
             )
         late = ctx.enter_context(tc.tile_pool(name="late", bufs=1))
         y_sb = [late.tile([P, S], F32, name="y%d" % t, align_bytes=64, offset=(t + 2) % PACK * 4 * S * 2) for t in range(PACK)]
@@ -131,7 +133,8 @@ def tile_picked_headmod_silu_po_kernel(
             nc.scalar.activation(sig[t][:, e0:e1], y_sb[t][:].indirect(take_sb[:, e0 // 16 : e1 // 16]), SIGMOID)
 
         first_product(0, slice(0, S // 2), "bank0", nc.scalar.copy)
-        first_product(0, slice(S // 2, S), "bank1", nc.scalar.copy)
+        first_product(0, slice(S // 2, 3 * S // 4), "bank3", nc.vector.tensor_copy)
+        first_product(0, slice(3 * S // 4, S), "bank1", nc.vector.tensor_copy)
         look_up(0, 0, V)
         for t in range(1, PACK):
             first_product(t, slice(0, S), "bank%d" % (1 + t % 2), nc.vector.tensor_copy if t == 1 else nc.scalar.copy)
@@ -142,6 +145,7 @@ def tile_picked_headmod_silu_po_kernel(
             w2_codes[:].rearrange("p (t m) -> p m t", t=PACK),
             w2_table[:].bitcast(U32).rearrange("p (m t) -> p m t", t=PACK),
         )
+
 
         z = late.tile([P, CHUNKS, PACK, CHUNK], BF16, name="z", align_bytes=64, offset=0)
 

@@ -171,7 +171,7 @@ def tile_picked_headmod_silu_po_kernel(
         update(0, 0, CHUNKS)
         update(1, 0, CHUNKS)
         scatter(3)
-        update(2, 0, 1)
+        update(2, 0, 2)
 
         z_grouped = [sb("z_grouped%d" % c, [P, CHUNK * PACK], BF16) for c in range(CHUNKS)]
         z_codes = [sb("z_codes%d" % c, [P, CHUNK], U32) for c in range(CHUNKS)]
@@ -192,16 +192,25 @@ def tile_picked_headmod_silu_po_kernel(
             )
 
         def group_z(c):
-            group(nc.scalar.copy if c % 2 == 1 else nc.vector.tensor_copy, z_grouped[c][:], z[:, c])
+            group(nc.scalar.copy if c in (1, 2) else nc.vector.tensor_copy, z_grouped[c][:], z[:, c])
+
+        parts = (
+            ((0, 1, 0, nc.scalar.copy), (1, 2, 3, nc.scalar.copy), (2, PACK, 4, nc.scalar.copy)),
+            ((0, 2, 5, nc.scalar.copy), (2, PACK, 6, nc.vector.tensor_copy)),
+        )
+        out_banks = {}
 
         def second_product(c):
             nc.vector.quantize_mx(out=z_codes[c][:].bitcast(FP8X4), scales=z_plane[c][:], in_=z_grouped[c][:])
-            parts = ((0, PACK, 4 + c),) if c > 0 else ((0, 2, 3), (2, PACK, 4))
-            for t0, t1, number in parts:
-                bank = psum.tile([P, PACK, CHUNK], F32, name="bank%d" % number)
+            half, first = divmod(c, 2)
+            staged = (res_first, res_last)[half]
+            for t0, t1, number, copy in parts[half]:
+                if first == 0:
+                    out_banks[number] = psum.tile([P, 2, 2 * CHUNK], F32, name="bank%d" % number)
+                bank = out_banks[number]
                 for t in range(t0, t1):
                     nc.tensor.matmul_mx(
-                        out=bank[:, t, :],
+                        out=bank[:, t - t0, first * CHUNK : (first + 1) * CHUNK],
                         lhsT=w2_codes[:, t * P : (t + 1) * P].bitcast(FP8X4),
                         lhsT_scale=w2_plane[:, t * P : (t + 1) * P],
                         rhs=z_codes[c][:].bitcast(FP8X4),
@@ -209,37 +218,38 @@ def tile_picked_headmod_silu_po_kernel(
                         start=True,
                         stop=True,
                     )
-                nc.scalar.copy(res[c][:, t0:t1, :], bank[:, t0:t1, :])
-                if c < 2:
-                    nc.sync.dma_start(out=out_rows[:, t0:t1, c * CHUNK : (c + 1) * CHUNK], in_=res[c][:, t0:t1, :])
-            if c == CHUNKS - 1:
-                nc.sync.dma_start(out=out_rows[:, :, 2 * CHUNK : S], in_=res_last[:])
+                if first == 1:
+                    copy(staged[:, t0:t1, :], bank[:, 0 : t1 - t0, :])
+                    nc.sync.dma_start(
+                        out=out_rows[:, t0:t1, half * 2 * CHUNK : (half + 1) * 2 * CHUNK], in_=staged[:, t0:t1, :]
+                    )
 
         def quantize_result(i):
             cols = slice(pieces[i][0] * CHUNK, pieces[i][1] * CHUNK)
             nc.vector.quantize_mx(out=res_codes[:, cols].bitcast(FP8X4), scales=res_plane[:, cols], in_=res_grouped[i][:])
 
         update(3, 0, 1)
-        update(2, 1, CHUNKS)
-        group_z(0)
         update(3, 1, 2)
+        group_z(0)
         group_z(1)
+        update(2, 2, CHUNKS)
         second_product(0)
         update(3, 2, 3)
+        group_z(2)
         second_product(1)
         update(3, 3, 4)
-        group_z(2)
         group_z(3)
         second_product(2)
         second_product(3)
         group(nc.vector.tensor_copy, res_grouped[0][:], res_first[:])
-        for i in range(1, len(pieces)):
-            group(nc.vector.tensor_copy, res_grouped[i][:], pieces[i][2])
-            quantize_result(i - 1)
-        quantize_result(len(pieces) - 1)
+        quantize_result(0)
+        group(nc.vector.tensor_copy, res_grouped[1][:], pieces[1][2])
+        group(nc.scalar.copy, res_grouped[2][:], pieces[2][2])
+        quantize_result(1)
+        quantize_result(2)
 
         out_words = out_1[0].rearrange("p c r -> p (c r)").bitcast(I32)
-        for cols in (slice(0, 3 * CHUNK), slice(3 * CHUNK, S)):
+        for cols in (slice(0, 2 * CHUNK), slice(2 * CHUNK, S)):
             nc.sync.dma_start(out=out_words[:, cols], in_=res_codes[:, cols].bitcast(I32))
         for q in range(QUADRANTS):
             nc.scalar.dma_start(

@@ -18,10 +18,19 @@ MULT = mybir.AluOpType.mult
 
 P = 128
 PACK = 4
-QUADRANTS = 4
+BLOCKS = 16
 QUADRANT = 32
+LIST_ROWS = 16
 CHUNK = 128
 CHUNKS = S // CHUNK
+HALF = S // 2
+
+VECTOR_COLUMNS = (88, 40)
+
+W2_WORDS_AT = 0
+W2_ROWS_AT = W2_WORDS_AT + 4 * N
+WT_AT = W2_ROWS_AT + 2 * N
+X_SCALES_AT = W2_ROWS_AT - N
 
 
 def tile_picked_headmod_silu_po_kernel(
@@ -30,31 +39,28 @@ def tile_picked_headmod_silu_po_kernel(
     nc = tc.nc
     with ExitStack() as ctx:
         pool = ctx.enter_context(tc.tile_pool(name="sbuf", bufs=1))
-        reuse = ctx.enter_context(tc.tile_pool(name="reuse", bufs=1))
+        shared = ctx.enter_context(tc.tile_pool(name="shared", bufs=1))
         psum = ctx.enter_context(tc.psum_pool(name="psum", bufs=1))
 
         def sb(name, shape, dtype):
             return pool.tile(shape, dtype, name=name, align_bytes=64)
 
         def move_scale_rows(plane, rows):
-            for q in range(QUADRANTS):
+            for q in range(P // QUADRANT):
                 nc.sync.dma_start(
                     out=plane[QUADRANT * q : QUADRANT * q + PACK, :].bitcast(I32),
                     in_=rows[PACK * q : PACK * q + PACK, :].bitcast(I32),
                 )
 
-        offs_sb = sb("offs_sb", [P, S // 16], U16)
-        take_sb = sb("take_sb", [P, V // 16], U16)
-        ROWS = 16
-        W2_ROWS_AT = 4 * N
-        WT_AT = W2_ROWS_AT + 2 * N
+        offs_sb = sb("offs_sb", [P, S // LIST_ROWS], U16)
+        take_sb = sb("take_sb", [P, V // LIST_ROWS], U16)
         warm = sb("warm", [P, 32], F32)
         warm_out = sb("warm_out", [P, 32], F32)
         x_table = sb("x_table", [P, T], I32)
-        x_scale_table = reuse.tile([P, T], U8, name="x_scale_table", align_bytes=64, offset=W2_ROWS_AT - N)
+        x_scale_table = shared.tile([P, T], U8, name="x_scale_table", align_bytes=64, offset=X_SCALES_AT)
         w1_raw = sb("w1_raw", [P, PACK, H], F32)
-        wt_sb = reuse.tile([P, V], F32, name="wt_sb", align_bytes=64, offset=WT_AT)
-        w2_table = reuse.tile([P, N], I32, name="w2_table", align_bytes=64, offset=0)
+        wt_sb = shared.tile([P, V], F32, name="wt_sb", align_bytes=64, offset=WT_AT)
+        w2_table = shared.tile([P, N], I32, name="w2_table", align_bytes=64, offset=W2_WORDS_AT)
         w2_scale_table = sb("w2_scale_table", [P, N], U8)
         gates = [sb("gates%d" % t, [P, S], F32) for t in range(PACK)]
         x_plane = sb("x_plane", [P, S], U8)
@@ -72,73 +78,81 @@ def tile_picked_headmod_silu_po_kernel(
         x_rows_hbm = x_words[0].rearrange("p c r -> p (c r)").bitcast(I32)
         nc.sync.dma_start(offs_sb[:], offs)
         nc.sync.dma_start(out=x_table[:, 0 : T // 2], in_=x_rows_hbm[:, 0 : T // 2])
-        nc.sync.dma_start(out=x_scale_table[0:ROWS, :].bitcast(I32), in_=x_scales[0].bitcast(I32))
-        nc.sync.dma_start(out=w2_scale_table[0:ROWS, :].bitcast(I32), in_=w2_scales[0].bitcast(I32))
+        nc.sync.dma_start(out=x_scale_table[0:BLOCKS, :].bitcast(I32), in_=x_scales[0].bitcast(I32))
+        nc.sync.dma_start(out=w2_scale_table[0:BLOCKS, :].bitcast(I32), in_=w2_scales[0].bitcast(I32))
         nc.sync.dma_start(out=x_table[:, T // 2 : T], in_=x_rows_hbm[:, T // 2 : T])
         nc.sync.dma_start(out=w1_raw[:], in_=w1.rearrange("(p j) c -> p j c", j=PACK))
         nc.sync.dma_start(take_sb[:], take)
 
-        x_rows = sb("x_rows", [P, S], U8)
-        nc.vector.tensor_copy(x_rows[:], x_scale_table[:].indirect(offs_sb[:]))
-        move_scale_rows(x_plane, x_rows)
+        x_scale_rows = sb("x_scale_rows", [P, S], U8)
+        nc.vector.tensor_copy(x_scale_rows[:], x_scale_table[:].indirect(offs_sb[:]))
+        move_scale_rows(x_plane, x_scale_rows)
+
         nc.sync.dma_start(out=w2_table[:], in_=w2_words[0].rearrange("p c r -> p (c r)").bitcast(I32))
         nc.sync.dma_start(out=wt_sb[:], in_=wt.rearrange("(p t) v -> p t v", t=PACK)[:, 0, :])
-        w2_rows = reuse.tile([P, N], U8, name="w2_rows", align_bytes=64, offset=W2_ROWS_AT)
+
+        w2_scale_rows = shared.tile([P, N], U8, name="w2_scale_rows", align_bytes=64, offset=W2_ROWS_AT)
         nc.vector.tensor_copy(
-            w2_rows[:].rearrange("p (t m) -> p t m", t=PACK),
+            w2_scale_rows[:].rearrange("p (t m) -> p t m", t=PACK),
             w2_scale_table[:].rearrange("p (m t) -> p t m", t=PACK),
         )
-        move_scale_rows(w2_plane, w2_rows)
+        move_scale_rows(w2_plane, w2_scale_rows)
 
         x_codes = sb("x_codes", [P, S], U32)
         nc.vector.tensor_copy(x_codes[:], x_table[:].bitcast(U32).indirect(offs_sb[:]))
 
-        w1_grouped = [sb("w1_grouped%d" % u, [P, H * 2], BF16) for u in range(2)]
+        w1_grouped = [sb("w1_grouped%d" % u, [P, 2 * P * PACK], BF16) for u in range(2)]
         w1_src = w1_raw[:].rearrange("p j (m u e) -> p u m j e", u=2, e=2)
-        w1_codes_all = sb("w1_codes_all", [P, H], U32)
-        w1_plane_all = sb("w1_plane_all", [P, H], U8)
-        w1_codes = [w1_codes_all[:, t * P : (t + 1) * P] for t in range(PACK)]
-        w1_plane = [w1_plane_all[:, t * P : (t + 1) * P] for t in range(PACK)]
-        for u, split in ((0, 88), (1, 40)):
-            view = w1_grouped[u][:].rearrange("p (e m j) -> p m j e", e=2, j=PACK)
-            nc.vector.tensor_copy(view[:, 0:split], w1_src[:, u, 0:split])
-            nc.scalar.copy(view[:, split:P], w1_src[:, u, split:P])
-        for t0, t1 in ((0, 1), (1, 2), (2, 4)):
+        w1_codes = sb("w1_codes", [P, H], U32)
+        w1_plane = sb("w1_plane", [P, H], U8)
+        for u, split in enumerate(VECTOR_COLUMNS):
+            w1_dst = w1_grouped[u][:].rearrange("p (e m j) -> p m j e", e=2, j=PACK)
+            nc.vector.tensor_copy(w1_dst[:, 0:split], w1_src[:, u, 0:split])
+            nc.scalar.copy(w1_dst[:, split:P], w1_src[:, u, split:P])
+        for t0, t1 in ((0, 1), (1, 2), (2, PACK)):
             nc.vector.quantize_mx(
-                out=w1_codes_all[:, t0 * P : t1 * P].bitcast(FP8X4),
-                scales=w1_plane_all[:, t0 * P : t1 * P],
+                out=w1_codes[:, t0 * P : t1 * P].bitcast(FP8X4),
+                scales=w1_plane[:, t0 * P : t1 * P],
                 in_=w1_grouped[t0 // 2][:, (t0 % 2) * P * PACK : (t0 % 2 + t1 - t0) * P * PACK],
             )
+
+        OVERLAID = 2
+        Z_BYTES = 2 * PACK * S
         late = ctx.enter_context(tc.tile_pool(name="late", bufs=1))
-        y_sb = [late.tile([P, S], F32, name="y%d" % t, align_bytes=64, offset=(t + 2) % PACK * 4 * S * 2) for t in range(PACK)]
-        y_banks = {}
+        y_sb = [
+            late.tile([P, S], F32, name="y%d" % t, align_bytes=64, offset=(t - OVERLAID) % PACK * Z_BYTES)
+            for t in range(PACK)
+        ]
         sig = [sb("sig%d" % t, [P, V], F32) for t in range(PACK)]
 
-        def first_product(t, cols, bank_name, copy):
-            y_bank = psum.tile([P, S], F32, name=bank_name)
-            y_banks[t] = y_bank
+        def first_product(t, cols, number, copy):
+            bank = psum.tile([P, S], F32, name="bank%d" % number)
             width = cols.stop - cols.start
             nc.tensor.matmul_mx(
-                out=y_bank[:, 0:width],
-                lhsT=w1_codes[t].bitcast(FP8X4),
-                lhsT_scale=w1_plane[t],
+                out=bank[:, 0:width],
+                lhsT=w1_codes[:, t * P : (t + 1) * P].bitcast(FP8X4),
+                lhsT_scale=w1_plane[:, t * P : (t + 1) * P],
                 rhs=x_codes[:, cols].bitcast(FP8X4),
                 rhs_scale=x_plane[:, cols],
                 start=True,
                 stop=True,
             )
-            copy(y_sb[t][:, cols], y_bank[:, 0:width])
+            copy(y_sb[t][:, cols], bank[:, 0:width])
+            return bank
 
-        def look_up(t, e0, e1):
-            nc.scalar.activation(sig[t][:, e0:e1], y_sb[t][:].indirect(take_sb[:, e0 // 16 : e1 // 16]), SIGMOID)
+        def look_up(t):
+            nc.scalar.activation(sig[t][:], y_sb[t][:].indirect(take_sb[:]), SIGMOID)
 
-        first_product(0, slice(0, S // 2), "bank0", nc.scalar.copy)
-        first_product(0, slice(S // 2, 3 * S // 4), "bank3", nc.vector.tensor_copy)
-        first_product(0, slice(3 * S // 4, S), "bank1", nc.vector.tensor_copy)
-        look_up(0, 0, V)
-        for t in range(1, PACK):
-            first_product(t, slice(0, S), "bank%d" % (1 + t % 2), nc.vector.tensor_copy if t == 1 else nc.scalar.copy)
-            look_up(t, 0, V)
+        first_product(0, slice(0, S // 2), 0, nc.scalar.copy)
+        first_product(0, slice(S // 2, 3 * S // 4), 3, nc.vector.tensor_copy)
+        first_product(0, slice(3 * S // 4, S), 1, nc.vector.tensor_copy)
+        look_up(0)
+        first_product(1, slice(0, S), 2, nc.vector.tensor_copy)
+        look_up(1)
+        y_overlaid_bank = first_product(OVERLAID, slice(0, S), 1, nc.scalar.copy)
+        look_up(OVERLAID)
+        first_product(3, slice(0, S), 2, nc.scalar.copy)
+        look_up(3)
 
         w2_codes = sb("w2_codes", [P, N], U32)
         nc.vector.tensor_copy(
@@ -146,21 +160,19 @@ def tile_picked_headmod_silu_po_kernel(
             w2_table[:].bitcast(U32).rearrange("p (m t) -> p m t", t=PACK),
         )
 
-
         z = late.tile([P, CHUNKS, PACK, CHUNK], BF16, name="z", align_bytes=64, offset=0)
 
-        def scatter(t, e0=0, e1=V):
-            nc.vector.tensor_tensor(
-                gates[t][:].indirect(take_sb[:, e0 // 16 : e1 // 16]), sig[t][:, e0:e1], wt_sb[:, e0:e1], MULT
-            )
+        def scatter(t):
+            nc.vector.tensor_tensor(gates[t][:].indirect(take_sb[:]), sig[t][:], wt_sb[:], MULT)
 
         def update(t, c0, c1):
             cols = slice(c0 * CHUNK, c1 * CHUNK)
+            y = y_overlaid_bank if t == OVERLAID else y_sb[t]
             nc.vector.scalar_tensor_tensor(
                 out=z[:, c0:c1, t, :],
                 in0=gates[t][:, cols].rearrange("p (c n) -> p c n", n=CHUNK),
                 scalar=1.0,
-                in1=(y_banks[t] if t == 2 else y_sb[t])[:, cols].rearrange("p (c n) -> p c n", n=CHUNK),
+                in1=y[:, cols].rearrange("p (c n) -> p c n", n=CHUNK),
                 op0=ADD,
                 op1=MULT,
             )
@@ -176,11 +188,9 @@ def tile_picked_headmod_silu_po_kernel(
         z_grouped = [sb("z_grouped%d" % c, [P, CHUNK * PACK], BF16) for c in range(CHUNKS)]
         z_codes = [sb("z_codes%d" % c, [P, CHUNK], U32) for c in range(CHUNKS)]
         z_plane = [sb("z_plane%d" % c, [P, CHUNK], U8) for c in range(CHUNKS)]
-        res_first = sb("res_first", [P, PACK, 2 * CHUNK], F32)
-        res_last = sb("res_last", [P, PACK, 2 * CHUNK], F32)
-        res = [pair[:, :, h * CHUNK : (h + 1) * CHUNK] for pair in (res_first, res_last) for h in range(2)]
-        pieces = ((0, 2, res_first[:]), (2, 3, res[2]), (3, 4, res[3]))
-        res_grouped = [sb("res_grouped%d" % c0, [P, (c1 - c0) * CHUNK * PACK], BF16) for c0, c1, src in pieces]
+        res = sb("res", [P, PACK, S], F32)
+        pieces = ((0, 2), (2, 3), (3, CHUNKS))
+        res_grouped = [sb("res_grouped%d" % c0, [P, (c1 - c0) * CHUNK * PACK], BF16) for c0, c1 in pieces]
         res_codes = sb("res_codes", [P, S], U32)
         res_plane = sb("res_plane", [P, S], U8)
         out_rows = out_0.rearrange("(p t) s -> p t s", t=PACK)
@@ -191,38 +201,45 @@ def tile_picked_headmod_silu_po_kernel(
                 src.rearrange("p t (n i) -> p n t i", i=4),
             )
 
-        def group_z(c):
-            group(nc.scalar.copy if c in (1, 2) else nc.vector.tensor_copy, z_grouped[c][:], z[:, c])
+        def group_z(c, copy):
+            group(copy, z_grouped[c][:], z[:, c])
+
+        def quantize_z(c):
+            nc.vector.quantize_mx(out=z_codes[c][:].bitcast(FP8X4), scales=z_plane[c][:], in_=z_grouped[c][:])
 
         parts = (
-            ((0, 1, 0, nc.scalar.copy), (1, 2, 3, nc.scalar.copy), (2, PACK, 4, nc.scalar.copy)),
-            ((0, 2, 5, nc.scalar.copy), (2, PACK, 6, nc.vector.tensor_copy)),
+            ((0, 1, 0, nc.scalar.copy), (1, 2, 3, nc.scalar.copy), (2, PACK, 4, nc.vector.tensor_copy)),
+            (
+                (0, 1, 5, nc.scalar.copy),
+                (1, 2, 6, nc.scalar.copy),
+                (2, 3, 7, nc.scalar.copy),
+                (3, PACK, 1, nc.vector.tensor_copy),
+            ),
         )
-        out_banks = {}
+        STORED_BY_HALVES = 2
 
-        def second_product(c):
-            nc.vector.quantize_mx(out=z_codes[c][:].bitcast(FP8X4), scales=z_plane[c][:], in_=z_grouped[c][:])
-            half, first = divmod(c, 2)
-            staged = (res_first, res_last)[half]
+        def second_product(half):
+            cols = slice(half * HALF, (half + 1) * HALF)
             for t0, t1, number, copy in parts[half]:
-                if first == 0:
-                    out_banks[number] = psum.tile([P, 2, 2 * CHUNK], F32, name="bank%d" % number)
-                bank = out_banks[number]
-                for t in range(t0, t1):
-                    nc.tensor.matmul_mx(
-                        out=bank[:, t - t0, first * CHUNK : (first + 1) * CHUNK],
-                        lhsT=w2_codes[:, t * P : (t + 1) * P].bitcast(FP8X4),
-                        lhsT_scale=w2_plane[:, t * P : (t + 1) * P],
-                        rhs=z_codes[c][:].bitcast(FP8X4),
-                        rhs_scale=z_plane[c][:],
-                        start=True,
-                        stop=True,
-                    )
-                if first == 1:
-                    copy(staged[:, t0:t1, :], bank[:, 0 : t1 - t0, :])
-                    nc.sync.dma_start(
-                        out=out_rows[:, t0:t1, half * 2 * CHUNK : (half + 1) * 2 * CHUNK], in_=staged[:, t0:t1, :]
-                    )
+                bank = psum.tile([P, 2, HALF], F32, name="bank%d" % number)
+                for place in range(HALF // CHUNK):
+                    c = half * HALF // CHUNK + place
+                    for t in range(t0, t1):
+                        nc.tensor.matmul_mx(
+                            out=bank[:, t - t0, place * CHUNK : (place + 1) * CHUNK],
+                            lhsT=w2_codes[:, t * P : (t + 1) * P].bitcast(FP8X4),
+                            lhsT_scale=w2_plane[:, t * P : (t + 1) * P],
+                            rhs=z_codes[c][:].bitcast(FP8X4),
+                            rhs_scale=z_plane[c][:],
+                            start=True,
+                            stop=True,
+                        )
+                copy(res[:, t0:t1, cols], bank[:, 0 : t1 - t0, :])
+                if t0 < STORED_BY_HALVES:
+                    nc.sync.dma_start(out=out_rows[:, t0:t1, cols], in_=res[:, t0:t1, cols])
+
+        def group_result(i, copy):
+            group(copy, res_grouped[i][:], res[:, :, pieces[i][0] * CHUNK : pieces[i][1] * CHUNK])
 
         def quantize_result(i):
             cols = slice(pieces[i][0] * CHUNK, pieces[i][1] * CHUNK)
@@ -230,28 +247,30 @@ def tile_picked_headmod_silu_po_kernel(
 
         update(3, 0, 1)
         update(3, 1, 2)
-        group_z(0)
-        group_z(1)
+        group_z(0, nc.vector.tensor_copy)
+        group_z(1, nc.scalar.copy)
         update(2, 2, CHUNKS)
-        second_product(0)
+        quantize_z(0)
         update(3, 2, 3)
-        group_z(2)
-        second_product(1)
-        update(3, 3, 4)
-        group_z(3)
-        second_product(2)
-        second_product(3)
-        group(nc.vector.tensor_copy, res_grouped[0][:], res_first[:])
+        group_z(2, nc.scalar.copy)
+        quantize_z(1)
+        update(3, 3, CHUNKS)
+        group_z(3, nc.vector.tensor_copy)
+        quantize_z(2)
+        quantize_z(3)
+        for half in range(S // HALF):
+            second_product(half)
+        nc.sync.dma_start(out=out_rows[:, STORED_BY_HALVES:PACK, :], in_=res[:, STORED_BY_HALVES:PACK, :])
+
+        group_result(0, nc.vector.tensor_copy)
         quantize_result(0)
-        group(nc.vector.tensor_copy, res_grouped[1][:], pieces[1][2])
-        group(nc.scalar.copy, res_grouped[2][:], pieces[2][2])
+        group_result(1, nc.vector.tensor_copy)
+        group_result(2, nc.scalar.copy)
         quantize_result(1)
         quantize_result(2)
 
-        out_words = out_1[0].rearrange("p c r -> p (c r)").bitcast(I32)
-        for cols in (slice(0, 2 * CHUNK), slice(2 * CHUNK, S)):
-            nc.sync.dma_start(out=out_words[:, cols], in_=res_codes[:, cols].bitcast(I32))
-        for q in range(QUADRANTS):
+        nc.sync.dma_start(out=out_1[0].rearrange("p c r -> p (c r)").bitcast(I32), in_=res_codes[:].bitcast(I32))
+        for q in range(P // QUADRANT):
             nc.scalar.dma_start(
                 out=out_2[0, PACK * q : PACK * q + PACK, :].bitcast(I32),
                 in_=res_plane[QUADRANT * q : QUADRANT * q + PACK, :].bitcast(I32),

@@ -116,14 +116,12 @@ def tile_picked_headmod_silu_po_kernel(
                 in_=w1_grouped[t0 // 2][:, (t0 % 2) * P * PACK : (t0 % 2 + t1 - t0) * P * PACK],
             )
 
-        OVERLAID = 2
-        Z_BYTES = 2 * PACK * S
         late = ctx.enter_context(tc.tile_pool(name="late", bufs=1))
         y_sb = [
-            late.tile([P, S], F32, name="y%d" % t, align_bytes=64, offset=(t - OVERLAID) % PACK * Z_BYTES)
-            for t in range(PACK)
+            late.tile([P, S], F32, name="y%d" % t, align_bytes=64, offset=(10, 12, 14, 2)[t] * 1024) for t in range(PACK)
         ]
-        sig = [sb("sig%d" % t, [P, V], F32) for t in range(PACK)]
+        sig = [late.tile([P, V], F32, name="sig%d" % t, align_bytes=64, offset=(6, 7, 0, 8)[t] * 1024) for t in range(PACK)]
+        y_banks = {}
 
         def first_product(t, cols, number, copy):
             bank = psum.tile([P, S], F32, name="bank%d" % number)
@@ -147,11 +145,11 @@ def tile_picked_headmod_silu_po_kernel(
         first_product(0, slice(S // 2, 3 * S // 4), 3, nc.vector.tensor_copy)
         first_product(0, slice(3 * S // 4, S), 1, nc.vector.tensor_copy)
         look_up(0)
-        first_product(1, slice(0, S), 2, nc.vector.tensor_copy)
+        y_banks[1] = first_product(1, slice(0, S), 2, nc.vector.tensor_copy)
         look_up(1)
-        y_overlaid_bank = first_product(OVERLAID, slice(0, S), 1, nc.scalar.copy)
-        look_up(OVERLAID)
-        first_product(3, slice(0, S), 2, nc.scalar.copy)
+        y_banks[2] = first_product(2, slice(0, S), 1, nc.scalar.copy)
+        look_up(2)
+        y_banks[3] = first_product(3, slice(0, S), 3, nc.scalar.copy)
         look_up(3)
 
         w2_codes = sb("w2_codes", [P, N], U32)
@@ -160,14 +158,14 @@ def tile_picked_headmod_silu_po_kernel(
             w2_table[:].bitcast(U32).rearrange("p (m t) -> p m t", t=PACK),
         )
 
-        z = late.tile([P, CHUNKS, PACK, CHUNK], BF16, name="z", align_bytes=64, offset=0)
+        z = late.tile([P, CHUNKS, PACK, CHUNK], BF16, name="z", align_bytes=64, offset=2 * 1024)
 
         def scatter(t):
             nc.vector.tensor_tensor(gates[t][:].indirect(take_sb[:]), sig[t][:], wt_sb[:], MULT)
 
         def update(t, c0, c1):
             cols = slice(c0 * CHUNK, c1 * CHUNK)
-            y = y_overlaid_bank if t == OVERLAID else y_sb[t]
+            y = y_banks[t]
             nc.vector.scalar_tensor_tensor(
                 out=z[:, c0:c1, t, :],
                 in0=gates[t][:, cols].rearrange("p (c n) -> p c n", n=CHUNK),
@@ -177,13 +175,18 @@ def tile_picked_headmod_silu_po_kernel(
                 op1=MULT,
             )
 
-        scatter(0)
-        scatter(1)
-        scatter(2)
-        update(0, 0, CHUNKS)
-        update(1, 0, CHUNKS)
-        scatter(3)
-        update(2, 0, 2)
+        for t in range(PACK):
+            scatter(t)
+        raised = late.tile([P, S], F32, name="raised", align_bytes=64, offset=0)
+        nc.scalar.activation(raised[:], gates[0][:], mybir.ActivationFunctionType.Copy, bias=1.0)
+        for half in range(2):
+            cols = slice(half * HALF, (half + 1) * HALF)
+            nc.gpsimd.tensor_tensor(
+                z[:, 2 * half : 2 * half + 2, 0, :],
+                raised[:, cols].rearrange("p (c n) -> p c n", n=CHUNK),
+                y_sb[0][:, cols].rearrange("p (c n) -> p c n", n=CHUNK),
+                MULT,
+            )
 
         z_grouped = [sb("z_grouped%d" % c, [P, CHUNK * PACK], BF16) for c in range(CHUNKS)]
         z_codes = [sb("z_codes%d" % c, [P, CHUNK], U32) for c in range(CHUNKS)]
@@ -208,12 +211,17 @@ def tile_picked_headmod_silu_po_kernel(
             nc.vector.quantize_mx(out=z_codes[c][:].bitcast(FP8X4), scales=z_plane[c][:], in_=z_grouped[c][:])
 
         parts = (
-            ((0, 1, 0, nc.scalar.copy), (1, 2, 3, nc.scalar.copy), (2, PACK, 4, nc.vector.tensor_copy)),
             (
-                (0, 1, 5, nc.scalar.copy),
-                (1, 2, 6, nc.scalar.copy),
-                (2, 3, 7, nc.scalar.copy),
-                (3, PACK, 1, nc.vector.tensor_copy),
+                (0, 1, 0, nc.scalar.copy),
+                (1, 2, 4, nc.scalar.copy),
+                (2, 3, 5, nc.scalar.copy),
+                (3, PACK, 6, nc.vector.tensor_copy),
+            ),
+            (
+                (0, 1, 7, nc.scalar.copy),
+                (1, 2, 2, nc.scalar.copy),
+                (2, 3, 1, nc.scalar.copy),
+                (3, PACK, 3, nc.vector.tensor_copy),
             ),
         )
         STORED_BY_HALVES = 2
@@ -245,19 +253,20 @@ def tile_picked_headmod_silu_po_kernel(
             cols = slice(pieces[i][0] * CHUNK, pieces[i][1] * CHUNK)
             nc.vector.quantize_mx(out=res_codes[:, cols].bitcast(FP8X4), scales=res_plane[:, cols], in_=res_grouped[i][:])
 
-        update(3, 0, 1)
-        update(3, 1, 2)
+        update(1, 0, 2)
+        update(2, 0, 2)
+        update(3, 0, 2)
+        update(1, 2, CHUNKS)
         group_z(0, nc.vector.tensor_copy)
         group_z(1, nc.scalar.copy)
         update(2, 2, CHUNKS)
         quantize_z(0)
-        update(3, 2, 3)
-        group_z(2, nc.scalar.copy)
+        update(3, 2, CHUNKS)
         quantize_z(1)
-        update(3, 3, CHUNKS)
+        group_z(2, nc.scalar.copy)
         group_z(3, nc.vector.tensor_copy)
-        quantize_z(2)
         quantize_z(3)
+        quantize_z(2)
         for half in range(S // HALF):
             second_product(half)
         nc.sync.dma_start(out=out_rows[:, STORED_BY_HALVES:PACK, :], in_=res[:, STORED_BY_HALVES:PACK, :])

@@ -1,6 +1,7 @@
 from contextlib import ExitStack
 
 import concourse.mybir as mybir
+from concourse.masks import make_identity
 
 K, T, S, V, H, N = 512, 2048, 512, 256, 512, 512
 FLOPS = 2 * K * H * S + 2 * H * N * S
@@ -12,25 +13,28 @@ U32 = mybir.dt.uint32
 U16 = mybir.dt.uint16
 U8 = mybir.dt.uint8
 FP8X4 = mybir.dt.float8_e4m3fn_x4
-SIGMOID = mybir.ActivationFunctionType.Sigmoid
+SILU = mybir.ActivationFunctionType.Silu
+COPY = mybir.ActivationFunctionType.Copy
 ADD = mybir.AluOpType.add
 MULT = mybir.AluOpType.mult
 
 P = 128
 PACK = 4
 BLOCKS = 16
+ROWS_AT = P - BLOCKS
 QUADRANT = 32
 LIST_ROWS = 16
 CHUNK = 128
 CHUNKS = S // CHUNK
 HALF = S // 2
 
-VECTOR_COLUMNS = (88, 40)
+VECTOR_COLUMNS = ((P, 0), (88, 40))
 
 W2_WORDS_AT = 0
 W2_ROWS_AT = W2_WORDS_AT + 4 * N
 WT_AT = W2_ROWS_AT + 2 * N
 X_SCALES_AT = W2_ROWS_AT - N
+W2_CODES_AT = 10 * N
 
 
 def tile_picked_headmod_silu_po_kernel(
@@ -49,7 +53,7 @@ def tile_picked_headmod_silu_po_kernel(
             for q in range(P // QUADRANT):
                 nc.sync.dma_start(
                     out=plane[QUADRANT * q : QUADRANT * q + PACK, :].bitcast(I32),
-                    in_=rows[PACK * q : PACK * q + PACK, :].bitcast(I32),
+                    in_=rows[ROWS_AT + PACK * q : ROWS_AT + PACK * q + PACK, :].bitcast(I32),
                 )
 
         offs_sb = sb("offs_sb", [P, S // LIST_ROWS], U16)
@@ -58,31 +62,38 @@ def tile_picked_headmod_silu_po_kernel(
         warm_out = sb("warm_out", [P, 32], F32)
         x_table = sb("x_table", [P, T], I32)
         x_scale_table = shared.tile([P, T], U8, name="x_scale_table", align_bytes=64, offset=X_SCALES_AT)
-        w1_raw = sb("w1_raw", [P, PACK, H], F32)
+        w1_raw = [sb("w1_raw%d" % a, [P, 2, H], F32) for a in range(2)]
         wt_sb = shared.tile([P, V], F32, name="wt_sb", align_bytes=64, offset=WT_AT)
         w2_table = shared.tile([P, N], I32, name="w2_table", align_bytes=64, offset=W2_WORDS_AT)
         w2_scale_table = sb("w2_scale_table", [P, N], U8)
-        gates = [sb("gates%d" % t, [P, S], F32) for t in range(PACK)]
+        d = [sb("d%d" % t, [P, S], F32) for t in range(PACK)]
         x_plane = sb("x_plane", [P, S], U8)
         w2_plane = sb("w2_plane", [P, N], U8)
 
-        nc.vector.memset(x_scale_table[:].bitcast(I32), 0)
-        nc.vector.memset(w2_scale_table[:].bitcast(I32), 0)
-        nc.vector.memset(warm[:], 0.0)
-        nc.scalar.activation(warm_out[:], warm[:], SIGMOID)
+        nc.vector.memset(x_scale_table[0:ROWS_AT, :].bitcast(I32), 0)
+        nc.vector.memset(w2_scale_table[0:ROWS_AT, :].bitcast(I32), 0)
         nc.vector.memset(x_plane[:].bitcast(I32), 0)
         nc.vector.memset(w2_plane[:].bitcast(I32), 0)
+        d_first = sb("d_first", [P, S], F32)
+        nc.vector.memset(d_first[:], 0.0)
         for t in range(PACK):
-            nc.vector.memset(gates[t][:], 0.0)
+            (nc.vector, nc.gpsimd)[t // 2].memset(d[t][:], 0.0)
+
+        identity = sb("identity", [P, P], F32)
+        identity_bf16 = sb("identity_bf16", [P, P], BF16)
+        make_identity(nc, identity[:])
+        make_identity(nc, identity_bf16[:])
 
         x_rows_hbm = x_words[0].rearrange("p c r -> p (c r)").bitcast(I32)
         nc.sync.dma_start(offs_sb[:], offs)
-        nc.sync.dma_start(out=x_table[:, 0 : T // 2], in_=x_rows_hbm[:, 0 : T // 2])
-        nc.sync.dma_start(out=x_scale_table[0:BLOCKS, :].bitcast(I32), in_=x_scales[0].bitcast(I32))
-        nc.sync.dma_start(out=w2_scale_table[0:BLOCKS, :].bitcast(I32), in_=w2_scales[0].bitcast(I32))
-        nc.sync.dma_start(out=x_table[:, T // 2 : T], in_=x_rows_hbm[:, T // 2 : T])
-        nc.sync.dma_start(out=w1_raw[:], in_=w1.rearrange("(p j) c -> p j c", j=PACK))
+        nc.scalar.dma_start(out=x_scale_table[ROWS_AT:P, :].bitcast(I32), in_=x_scales[0].bitcast(I32))
+        nc.scalar.dma_start(out=w2_scale_table[ROWS_AT:P, :].bitcast(I32), in_=w2_scales[0].bitcast(I32))
+        nc.sync.dma_start(out=x_table[:], in_=x_rows_hbm)
+        for a in range(2):
+            nc.sync.dma_start(out=w1_raw[a][:], in_=w1.rearrange("(p a j) c -> p a j c", a=2, j=2)[:, a])
         nc.sync.dma_start(take_sb[:], take)
+        nc.vector.memset(warm[:], 0.0)
+        nc.scalar.activation(warm_out[:], warm[:], SILU)
 
         x_scale_rows = sb("x_scale_rows", [P, S], U8)
         nc.vector.tensor_copy(x_scale_rows[:], x_scale_table[:].indirect(offs_sb[:]))
@@ -101,14 +112,20 @@ def tile_picked_headmod_silu_po_kernel(
         x_codes = sb("x_codes", [P, S], U32)
         nc.vector.tensor_copy(x_codes[:], x_table[:].bitcast(U32).indirect(offs_sb[:]))
 
-        w1_grouped = [sb("w1_grouped%d" % u, [P, 2 * P * PACK], BF16) for u in range(2)]
-        w1_src = w1_raw[:].rearrange("p j (m u e) -> p u m j e", u=2, e=2)
+        w1_grouped = [
+            shared.tile([P, 2 * P * PACK], BF16, name="w1_grouped0", align_bytes=64, offset=W2_CODES_AT),
+            sb("w1_grouped1", [P, 2 * P * PACK], BF16),
+        ]
         w1_codes = sb("w1_codes", [P, H], U32)
         w1_plane = sb("w1_plane", [P, H], U8)
-        for u, split in enumerate(VECTOR_COLUMNS):
-            w1_dst = w1_grouped[u][:].rearrange("p (e m j) -> p m j e", e=2, j=PACK)
-            nc.vector.tensor_copy(w1_dst[:, 0:split], w1_src[:, u, 0:split])
-            nc.scalar.copy(w1_dst[:, split:P], w1_src[:, u, split:P])
+        for a in range(2):
+            w1_src = w1_raw[a][:].rearrange("p j (m u e) -> p u m j e", u=2, e=2)
+            for u, split in enumerate(VECTOR_COLUMNS[a]):
+                w1_dst = w1_grouped[u][:].rearrange("p (e m a j) -> p a m j e", e=2, a=2, j=2)[:, a]
+                if split:
+                    nc.vector.tensor_copy(w1_dst[:, 0:split], w1_src[:, u, 0:split])
+                if split < P:
+                    nc.scalar.copy(w1_dst[:, split:P], w1_src[:, u, split:P])
         for t0, t1 in ((0, 1), (1, 2), (2, PACK)):
             nc.vector.quantize_mx(
                 out=w1_codes[:, t0 * P : t1 * P].bitcast(FP8X4),
@@ -117,17 +134,16 @@ def tile_picked_headmod_silu_po_kernel(
             )
 
         late = ctx.enter_context(tc.tile_pool(name="late", bufs=1))
-        y_sb = [
-            late.tile([P, S], F32, name="y%d" % t, align_bytes=64, offset=(10, 12, 14, 2)[t] * 1024) for t in range(PACK)
-        ]
-        sig = [late.tile([P, V], F32, name="sig%d" % t, align_bytes=64, offset=(6, 7, 0, 8)[t] * 1024) for t in range(PACK)]
-        y_banks = {}
 
-        def first_product(t, cols, number, copy):
-            bank = psum.tile([P, S], F32, name="bank%d" % number)
-            width = cols.stop - cols.start
+        def at(name, shape, dtype, offset):
+            return late.tile(shape, dtype, name=name, align_bytes=64, offset=offset)
+
+        def bank(number, shape, dtype=F32):
+            return psum.tile(shape, dtype, name="bank%d" % number)
+
+        def first_pass(t, cols, out):
             nc.tensor.matmul_mx(
-                out=bank[:, 0:width],
+                out=out,
                 lhsT=w1_codes[:, t * P : (t + 1) * P].bitcast(FP8X4),
                 lhsT_scale=w1_plane[:, t * P : (t + 1) * P],
                 rhs=x_codes[:, cols].bitcast(FP8X4),
@@ -135,60 +151,113 @@ def tile_picked_headmod_silu_po_kernel(
                 start=True,
                 stop=True,
             )
-            copy(y_sb[t][:, cols], bank[:, 0:width])
-            return bank
 
-        def look_up(t):
-            nc.scalar.activation(sig[t][:], y_sb[t][:].indirect(take_sb[:]), SIGMOID)
+        def first_product(t, cols, number):
+            out = bank(number, [P, cols.stop - cols.start])
+            first_pass(t, cols, out[:])
+            return out
 
-        first_product(0, slice(0, S // 2), 0, nc.scalar.copy)
-        first_product(0, slice(S // 2, 3 * S // 4), 3, nc.vector.tensor_copy)
-        first_product(0, slice(3 * S // 4, S), 1, nc.vector.tensor_copy)
-        look_up(0)
-        y_banks[1] = first_product(1, slice(0, S), 2, nc.vector.tensor_copy)
-        look_up(1)
-        y_banks[2] = first_product(2, slice(0, S), 1, nc.scalar.copy)
-        look_up(2)
-        y_banks[3] = first_product(3, slice(0, S), 3, nc.scalar.copy)
-        look_up(3)
+        silu_y = [at("silu_y%d" % t, [P, S], F32, (0, 5, 4, 6)[t] * 1024) for t in range(PACK)]
+        taken = [sb("taken%d" % t, [P, V], F32) for t in range(PACK)]
+        y0_sb = sb("y0", [P, S], F32)
+        y1_sb = at("y1", [P, S], F32, 1024)
 
-        w2_codes = sb("w2_codes", [P, N], U32)
+        def entries(v0, v1):
+            return take_sb[:, v0 // LIST_ROWS : v1 // LIST_ROWS]
+
+        def look_up(t, v0, v1):
+            nc.scalar.activation(taken[t][:, v0:v1], silu_y[t][:].indirect(entries(v0, v1)), COPY)
+
+        def scatter(t, v0, v1, window=None):
+            window = d[t] if window is None else window
+            nc.vector.tensor_tensor(window[:].indirect(entries(v0, v1)), taken[t][:, v0:v1], wt_sb[:, v0:v1], MULT)
+
+        halves = [slice(0, HALF), slice(HALF, S)]
+        y0_banks = [first_product(0, halves[h], h) for h in range(2)]
+        for h in range(2):
+            nc.scalar.activation(silu_y[0][:, halves[h]], y0_banks[h][:], SILU)
+        look_up(0, 0, V // 2)
+        look_up(0, V // 2, V)
+
+        for h in range(2):
+            nc.vector.tensor_copy(y0_sb[:, halves[h]], y0_banks[h][:])
+        scatter(0, 0, V // 2, d_first)
+        scatter(0, V // 2, V)
+        w2_codes = shared.tile([P, N], U32, name="w2_codes", align_bytes=64, offset=W2_CODES_AT)
         nc.vector.tensor_copy(
             w2_codes[:].rearrange("p (t m) -> p m t", t=PACK),
             w2_table[:].bitcast(U32).rearrange("p (m t) -> p m t", t=PACK),
         )
+        y1_cols = (slice(0, S - CHUNK), slice(S - CHUNK, S))
+        y1_banks = [bank(2, [P, S - CHUNK])]
+        for cols in (slice(0, HALF), slice(HALF, S - CHUNK)):
+            first_pass(1, cols, y1_banks[0][:, cols])
+        y1_banks.append(first_product(1, y1_cols[1], 0))
+        mixed = bank(3, [P, 2, HALF])
+        last = bank(7, [P, 2, HALF])
+        y_halves = {2: [bank(1, [P, HALF])[:], mixed[:, 0, :]], 3: [mixed[:, 1, :], last[:, 0, :]]}
+        for t in range(2, PACK):
+            for h in range(2):
+                first_pass(t, halves[h], y_halves[t][h])
+        for h in range(2):
+            nc.scalar.activation(silu_y[1][:, y1_cols[h]], y1_banks[h][:], SILU)
+        look_up(1, 0, V)
+        scatter(1, 0, V)
+        for h in range(2):
+            nc.scalar.copy(y1_sb[:, y1_cols[h]], y1_banks[h][:])
+        for h in range(2):
+            nc.scalar.activation(silu_y[2][:, halves[h]], y_halves[2][h], SILU)
+        look_up(2, 0, V)
+        scatter(2, 0, V)
+        for h in range(2):
+            nc.scalar.activation(silu_y[3][:, halves[h]], y_halves[3][h], SILU)
+        look_up(3, 0, V)
+        scatter(3, 0, V)
 
-        z = late.tile([P, CHUNKS, PACK, CHUNK], BF16, name="z", align_bytes=64, offset=2 * 1024)
+        z = at("z", [P, CHUNKS, PACK, CHUNK], BF16, 7680)
 
-        def scatter(t):
-            nc.vector.tensor_tensor(gates[t][:].indirect(take_sb[:]), sig[t][:], wt_sb[:], MULT)
+        def turned_sum(terms, number):
+            out = bank(number, [P, CHUNKS, P])
+            for i, src in enumerate(terms):
+                for c in range(CHUNKS):
+                    nc.tensor.matmul(
+                        out[:, c, :],
+                        src[c],
+                        identity[:],
+                        start=(i == 0 and c == 0),
+                        stop=(i == len(terms) - 1 and c == CHUNKS - 1),
+                        is_transpose=True,
+                    )
+            return out
+
+        def chunks(tile):
+            return [tile[:, c0 : c0 + CHUNK] for c0 in range(0, tile.shape[1], CHUNK)]
+
+        turned = [
+            turned_sum((chunks(y0_sb), chunks(d_first), chunks(d[0])), 4),
+            turned_sum((chunks(d[1]), chunks(y1_sb)), 5),
+        ]
+        z_turned = [at("z_turned%d" % t, [P, CHUNKS, P], BF16, (4096, 6656)[t]) for t in range(2)]
+        for t in range(2):
+            nc.scalar.copy(z_turned[t][:], turned[t][:])
+        for t in range(2):
+            words = (bank(6, [P, HALF])[:], last[:, 1, :])[t] if t == 0 else last[:, 1, :]
+            back = words.bitcast(BF16).rearrange("p (c n) -> p c n", n=CHUNK)
+            for c in range(CHUNKS):
+                nc.tensor.transpose(back[:, c, :], z_turned[t][:, c, :], identity_bf16[:])
+            nc.scalar.copy(z[:, :, t, :], back)
+
 
         def update(t, c0, c1):
             cols = slice(c0 * CHUNK, c1 * CHUNK)
-            y = y_banks[t]
-            nc.vector.scalar_tensor_tensor(
-                out=z[:, c0:c1, t, :],
-                in0=gates[t][:, cols].rearrange("p (c n) -> p c n", n=CHUNK),
-                scalar=1.0,
-                in1=y[:, cols].rearrange("p (c n) -> p c n", n=CHUNK),
-                op0=ADD,
-                op1=MULT,
+            nc.vector.tensor_tensor(
+                z[:, c0:c1, t, :],
+                d[t][:, cols].rearrange("p (c n) -> p c n", n=CHUNK),
+                y_halves[t][c0 // 2].rearrange("p (c n) -> p c n", n=CHUNK),
+                ADD,
             )
 
-        for t in range(PACK):
-            scatter(t)
-        raised = late.tile([P, S], F32, name="raised", align_bytes=64, offset=0)
-        nc.scalar.activation(raised[:], gates[0][:], mybir.ActivationFunctionType.Copy, bias=1.0)
-        for half in range(2):
-            cols = slice(half * HALF, (half + 1) * HALF)
-            nc.gpsimd.tensor_tensor(
-                z[:, 2 * half : 2 * half + 2, 0, :],
-                raised[:, cols].rearrange("p (c n) -> p c n", n=CHUNK),
-                y_sb[0][:, cols].rearrange("p (c n) -> p c n", n=CHUNK),
-                MULT,
-            )
-
-        z_grouped = [sb("z_grouped%d" % c, [P, CHUNK * PACK], BF16) for c in range(CHUNKS)]
+        z_grouped = [at("z_grouped%d" % c, [P, CHUNK * PACK], BF16, (12, 13, 14, 13)[c] * 1024) for c in range(CHUNKS)]
         z_codes = [sb("z_codes%d" % c, [P, CHUNK], U32) for c in range(CHUNKS)]
         z_plane = [sb("z_plane%d" % c, [P, CHUNK], U8) for c in range(CHUNKS)]
         res = sb("res", [P, PACK, S], F32)
@@ -212,16 +281,16 @@ def tile_picked_headmod_silu_po_kernel(
 
         parts = (
             (
-                (0, 1, 0, nc.scalar.copy),
-                (1, 2, 4, nc.scalar.copy),
-                (2, 3, 5, nc.scalar.copy),
-                (3, PACK, 6, nc.vector.tensor_copy),
+                (0, 1, 2, nc.scalar.copy),
+                (1, 2, 0, nc.scalar.copy),
+                (2, 3, 4, nc.scalar.copy),
+                (3, PACK, 5, nc.vector.tensor_copy),
             ),
             (
-                (0, 1, 7, nc.scalar.copy),
-                (1, 2, 2, nc.scalar.copy),
-                (2, 3, 1, nc.scalar.copy),
-                (3, PACK, 3, nc.vector.tensor_copy),
+                (0, 1, 6, nc.scalar.copy),
+                (1, 2, 1, nc.scalar.copy),
+                (2, 3, 3, nc.scalar.copy),
+                (3, PACK, 7, nc.vector.tensor_copy),
             ),
         )
         STORED_BY_HALVES = 2
@@ -229,12 +298,12 @@ def tile_picked_headmod_silu_po_kernel(
         def second_product(half):
             cols = slice(half * HALF, (half + 1) * HALF)
             for t0, t1, number, copy in parts[half]:
-                bank = psum.tile([P, 2, HALF], F32, name="bank%d" % number)
+                acc = bank(number, [P, 2, HALF])
                 for place in range(HALF // CHUNK):
                     c = half * HALF // CHUNK + place
                     for t in range(t0, t1):
                         nc.tensor.matmul_mx(
-                            out=bank[:, t - t0, place * CHUNK : (place + 1) * CHUNK],
+                            out=acc[:, t - t0, place * CHUNK : (place + 1) * CHUNK],
                             lhsT=w2_codes[:, t * P : (t + 1) * P].bitcast(FP8X4),
                             lhsT_scale=w2_plane[:, t * P : (t + 1) * P],
                             rhs=z_codes[c][:].bitcast(FP8X4),
@@ -242,7 +311,7 @@ def tile_picked_headmod_silu_po_kernel(
                             start=True,
                             stop=True,
                         )
-                copy(res[:, t0:t1, cols], bank[:, 0 : t1 - t0, :])
+                copy(res[:, t0:t1, cols], acc[:, 0 : t1 - t0, :])
                 if t0 < STORED_BY_HALVES:
                     nc.sync.dma_start(out=out_rows[:, t0:t1, cols], in_=res[:, t0:t1, cols])
 
@@ -253,16 +322,14 @@ def tile_picked_headmod_silu_po_kernel(
             cols = slice(pieces[i][0] * CHUNK, pieces[i][1] * CHUNK)
             nc.vector.quantize_mx(out=res_codes[:, cols].bitcast(FP8X4), scales=res_plane[:, cols], in_=res_grouped[i][:])
 
-        update(1, 0, 2)
         update(2, 0, 2)
         update(3, 0, 2)
-        update(1, 2, CHUNKS)
-        group_z(0, nc.vector.tensor_copy)
-        group_z(1, nc.scalar.copy)
         update(2, 2, CHUNKS)
-        quantize_z(0)
+        group_z(0, nc.scalar.copy)
+        group_z(1, nc.vector.tensor_copy)
         update(3, 2, CHUNKS)
         quantize_z(1)
+        quantize_z(0)
         group_z(2, nc.scalar.copy)
         group_z(3, nc.vector.tensor_copy)
         quantize_z(3)

@@ -261,8 +261,7 @@ def tile_picked_headmod_silu_po_kernel(
         z_codes = [sb("z_codes%d" % c, [P, CHUNK], U32) for c in range(CHUNKS)]
         z_plane = [sb("z_plane%d" % c, [P, CHUNK], U8) for c in range(CHUNKS)]
         res = sb("res", [P, PACK, S], F32)
-        pieces = ((0, 2), (2, 3), (3, CHUNKS))
-        res_grouped = [sb("res_grouped%d" % c0, [P, (c1 - c0) * CHUNK * PACK], BF16) for c0, c1 in pieces]
+        res_grouped = sb("res_grouped", [P, S * PACK], BF16)
         res_codes = sb("res_codes", [P, S], U32)
         res_plane = sb("res_plane", [P, S], U8)
         out_rows = out_0.rearrange("(p t) s -> p t s", t=PACK)
@@ -279,48 +278,45 @@ def tile_picked_headmod_silu_po_kernel(
         def quantize_z(c):
             nc.vector.quantize_mx(out=z_codes[c][:].bitcast(FP8X4), scales=z_plane[c][:], in_=z_grouped[c][:])
 
-        parts = (
-            (
-                (0, 1, 2, nc.scalar.copy),
-                (1, 2, 0, nc.scalar.copy),
-                (2, 3, 4, nc.scalar.copy),
-                (3, PACK, 5, nc.vector.tensor_copy),
-            ),
-            (
-                (0, 1, 6, nc.scalar.copy),
-                (1, 2, 1, nc.scalar.copy),
-                (2, 3, 3, nc.scalar.copy),
-                (3, PACK, 7, nc.vector.tensor_copy),
-            ),
-        )
-        STORED_BY_HALVES = 2
+        def second_product(c, u, acc):
+            for e in range(2):
+                t = 2 * u + e
+                nc.tensor.matmul_mx(
+                    out=acc[:, e, :],
+                    lhsT=w2_codes[:, t * P : (t + 1) * P].bitcast(FP8X4),
+                    lhsT_scale=w2_plane[:, t * P : (t + 1) * P],
+                    rhs=z_codes[c][:].bitcast(FP8X4),
+                    rhs_scale=z_plane[c][:],
+                    start=True,
+                    stop=True,
+                )
 
-        def second_product(half):
-            cols = slice(half * HALF, (half + 1) * HALF)
-            for t0, t1, number, copy in parts[half]:
-                acc = bank(number, [P, 2, HALF])
-                for place in range(HALF // CHUNK):
-                    c = half * HALF // CHUNK + place
-                    for t in range(t0, t1):
-                        nc.tensor.matmul_mx(
-                            out=acc[:, t - t0, place * CHUNK : (place + 1) * CHUNK],
-                            lhsT=w2_codes[:, t * P : (t + 1) * P].bitcast(FP8X4),
-                            lhsT_scale=w2_plane[:, t * P : (t + 1) * P],
-                            rhs=z_codes[c][:].bitcast(FP8X4),
-                            rhs_scale=z_plane[c][:],
-                            start=True,
-                            stop=True,
-                        )
-                copy(res[:, t0:t1, cols], acc[:, 0 : t1 - t0, :])
-                if t0 < STORED_BY_HALVES:
-                    nc.sync.dma_start(out=out_rows[:, t0:t1, cols], in_=res[:, t0:t1, cols])
+        def empty(c, u, acc, copy):
+            copy(res[:, 2 * u : 2 * u + 2, c * CHUNK : (c + 1) * CHUNK], acc)
 
-        def group_result(i, copy):
-            group(copy, res_grouped[i][:], res[:, :, pieces[i][0] * CHUNK : pieces[i][1] * CHUNK])
+        def half_product(first, second, numbers):
+            alone = bank(numbers[0], [P, 2, CHUNK])
+            both = bank(numbers[1], [P, PACK, CHUNK])
+            final = bank(numbers[2], [P, 2, CHUNK])
+            second_product(first, 0, alone)
+            empty(first, 0, alone[:], nc.scalar.copy)
+            second_product(first, 1, both[:, 0:2, :])
+            second_product(second, 0, both[:, 2:PACK, :])
+            empty(second, 0, both[:, 2:PACK, :], nc.scalar.copy)
+            empty(first, 1, both[:, 0:2, :], nc.scalar.copy)
+            second_product(second, 1, final)
+            empty(second, 1, final[:], nc.vector.tensor_copy)
 
-        def quantize_result(i):
-            cols = slice(pieces[i][0] * CHUNK, pieces[i][1] * CHUNK)
-            nc.vector.quantize_mx(out=res_codes[:, cols].bitcast(FP8X4), scales=res_plane[:, cols], in_=res_grouped[i][:])
+        def group_result(c, copy):
+            group(copy, res_grouped[:, c * CHUNK * PACK : (c + 1) * CHUNK * PACK], res[:, :, c * CHUNK : (c + 1) * CHUNK])
+
+        def quantize_result(c0, c1):
+            cols = slice(c0 * CHUNK, c1 * CHUNK)
+            nc.vector.quantize_mx(
+                out=res_codes[:, cols].bitcast(FP8X4),
+                scales=res_plane[:, cols],
+                in_=res_grouped[:, c0 * CHUNK * PACK : c1 * CHUNK * PACK],
+            )
 
         update(2, 0, 2)
         update(3, 0, 2)
@@ -334,16 +330,24 @@ def tile_picked_headmod_silu_po_kernel(
         group_z(3, nc.vector.tensor_copy)
         quantize_z(3)
         quantize_z(2)
-        for half in range(S // HALF):
-            second_product(half)
-        nc.sync.dma_start(out=out_rows[:, STORED_BY_HALVES:PACK, :], in_=res[:, STORED_BY_HALVES:PACK, :])
+        half_product(1, 0, (2, 0, 4))
+        for u in range(2):
+            nc.sync.dma_start(out=out_rows[:, 2 * u : 2 * u + 2, halves[0]], in_=res[:, 2 * u : 2 * u + 2, halves[0]])
+        for c, numbers, last_copy in ((3, (6, 1), nc.scalar.copy), (2, (3, 7), nc.vector.tensor_copy)):
+            for u, copy in enumerate((nc.scalar.copy, last_copy)):
+                acc = bank(numbers[u], [P, 2, CHUNK])
+                second_product(c, u, acc)
+                empty(c, u, acc[:], copy)
+        for u in range(2):
+            nc.sync.dma_start(out=out_rows[:, 2 * u : 2 * u + 2, halves[1]], in_=res[:, 2 * u : 2 * u + 2, halves[1]])
 
-        group_result(0, nc.vector.tensor_copy)
-        quantize_result(0)
         group_result(1, nc.vector.tensor_copy)
-        group_result(2, nc.scalar.copy)
-        quantize_result(1)
-        quantize_result(2)
+        group_result(0, nc.vector.tensor_copy)
+        quantize_result(0, 2)
+        group_result(3, nc.scalar.copy)
+        group_result(2, nc.vector.tensor_copy)
+        quantize_result(3, 4)
+        quantize_result(2, 3)
 
         nc.sync.dma_start(out=out_1[0].rearrange("p c r -> p (c r)").bitcast(I32), in_=res_codes[:].bitcast(I32))
         for q in range(P // QUADRANT):

@@ -235,7 +235,7 @@ def tile_picked_headmod_silu_po_kernel(
 
         turned = [
             turned_sum((chunks(y0_sb), chunks(d_first), chunks(d[0])), 4),
-            turned_sum((chunks(d[1]), chunks(y1_sb)), 5),
+            turned_sum((chunks(y1_sb), chunks(d[1])), 5),
         ]
         z_turned = [at("z_turned%d" % t, [P, CHUNKS, P], BF16, (4096, 6656)[t]) for t in range(2)]
         for t in range(2):
@@ -349,9 +349,11 @@ def tile_picked_headmod_silu_po_kernel(
         quantize_result(3, 4)
         quantize_result(2, 3)
 
-        nc.sync.dma_start(out=out_1[0].rearrange("p c r -> p (c r)").bitcast(I32), in_=res_codes[:].bitcast(I32))
+        words_out = out_1[0].rearrange("p c r -> p (c r)").bitcast(I32)
+        for cols in halves:
+            nc.sync.dma_start(out=words_out[:, cols], in_=res_codes[:, cols].bitcast(I32))
         for q in range(P // QUADRANT):
-            nc.scalar.dma_start(
+            (nc.scalar, nc.sync)[q // 2].dma_start(
                 out=out_2[0, PACK * q : PACK * q + PACK, :].bitcast(I32),
                 in_=res_plane[QUADRANT * q : QUADRANT * q + PACK, :].bitcast(I32),
             )

from contextlib import ExitStack

import concourse.mybir as mybir
from concourse.masks import make_identity

K, T, S, V, H, N = 512, 2048, 512, 256, 512, 512
FLOPS = 2 * K * H * S + 2 * H * N * S

F32 = mybir.dt.float32
BF16 = mybir.dt.bfloat16
I32 = mybir.dt.int32
U32 = mybir.dt.uint32
U16 = mybir.dt.uint16
U8 = mybir.dt.uint8
FP8X4 = mybir.dt.float8_e4m3fn_x4
SILU = mybir.ActivationFunctionType.Silu
COPY = mybir.ActivationFunctionType.Copy
ADD = mybir.AluOpType.add
MULT = mybir.AluOpType.mult

P = 128
PACK = 4
BLOCKS = 16
ROWS_AT = P - BLOCKS
QUADRANT = 32
LIST_ROWS = 16
CHUNK = 128
CHUNKS = S // CHUNK
HALF = S // 2

VECTOR_COLUMNS = ((P, 0), (88, 40))

W2_WORDS_AT = 0
W2_ROWS_AT = W2_WORDS_AT + 4 * N
WT_AT = W2_ROWS_AT + 2 * N
X_SCALES_AT = W2_ROWS_AT - N
W2_CODES_AT = 10 * N


def tile_picked_headmod_silu_po_kernel(
    tc, x_words, x_scales, w1, wt, w2_words, w2_scales, offs, take, out_0, out_1, out_2
):
    nc = tc.nc
    with ExitStack() as ctx:
        pool = ctx.enter_context(tc.tile_pool(name="sbuf", bufs=1))
        shared = ctx.enter_context(tc.tile_pool(name="shared", bufs=1))
        psum = ctx.enter_context(tc.psum_pool(name="psum", bufs=1))

        def sb(name, shape, dtype):
            return pool.tile(shape, dtype, name=name, align_bytes=64)

        def move_scale_rows(plane, rows):
            for q in range(P // QUADRANT):
                nc.sync.dma_start(
                    out=plane[QUADRANT * q : QUADRANT * q + PACK, :].bitcast(I32),
                    in_=rows[ROWS_AT + PACK * q : ROWS_AT + PACK * q + PACK, :].bitcast(I32),
                )

        offs_sb = sb("offs_sb", [P, S // LIST_ROWS], U16)
        take_sb = sb("take_sb", [P, V // LIST_ROWS], U16)
        warm = sb("warm", [P, 32], F32)
        warm_out = sb("warm_out", [P, 32], F32)
        x_table = sb("x_table", [P, T], I32)
        x_scale_table = shared.tile([P, T], U8, name="x_scale_table", align_bytes=64, offset=X_SCALES_AT)
        w1_raw = [sb("w1_raw%d" % a, [P, 2, H], F32) for a in range(2)]
        wt_sb = shared.tile([P, V], F32, name="wt_sb", align_bytes=64, offset=WT_AT)
        w2_table = shared.tile([P, N], I32, name="w2_table", align_bytes=64, offset=W2_WORDS_AT)
        w2_scale_table = sb("w2_scale_table", [P, N], U8)
        d = [sb("d%d" % t, [P, S], F32) for t in range(PACK)]
        x_plane = sb("x_plane", [P, S], U8)
        w2_plane = sb("w2_plane", [P, N], U8)

        nc.vector.memset(x_scale_table[0:ROWS_AT, :].bitcast(I32), 0)
        nc.vector.memset(w2_scale_table[0:ROWS_AT, :].bitcast(I32), 0)
        nc.vector.memset(x_plane[:].bitcast(I32), 0)
        nc.vector.memset(w2_plane[:].bitcast(I32), 0)
        d_first = sb("d_first", [P, S], F32)
        nc.vector.memset(d_first[:], 0.0)
        for t in range(PACK):
            (nc.vector, nc.gpsimd)[t // 2].memset(d[t][:], 0.0)

        identity = sb("identity", [P, P], F32)
        identity_bf16 = sb("identity_bf16", [P, P], BF16)
        make_identity(nc, identity[:])
        make_identity(nc, identity_bf16[:])

        x_rows_hbm = x_words[0].rearrange("p c r -> p (c r)").bitcast(I32)
        nc.sync.dma_start(offs_sb[:], offs)
        nc.scalar.dma_start(out=x_scale_table[ROWS_AT:P, :].bitcast(I32), in_=x_scales[0].bitcast(I32))
        nc.scalar.dma_start(out=w2_scale_table[ROWS_AT:P, :].bitcast(I32), in_=w2_scales[0].bitcast(I32))
        nc.sync.dma_start(out=x_table[:], in_=x_rows_hbm)
        for a in range(2):
            nc.sync.dma_start(out=w1_raw[a][:], in_=w1.rearrange("(p a j) c -> p a j c", a=2, j=2)[:, a])
        nc.sync.dma_start(take_sb[:], take)
        nc.vector.memset(warm[:], 0.0)
        nc.scalar.activation(warm_out[:], warm[:], SILU)

        x_scale_rows = sb("x_scale_rows", [P, S], U8)
        nc.vector.tensor_copy(x_scale_rows[:], x_scale_table[:].indirect(offs_sb[:]))
        move_scale_rows(x_plane, x_scale_rows)

        nc.sync.dma_start(out=w2_table[:], in_=w2_words[0].rearrange("p c r -> p (c r)").bitcast(I32))
        nc.sync.dma_start(out=wt_sb[:], in_=wt.rearrange("(p t) v -> p t v", t=PACK)[:, 0, :])

        w2_scale_rows = shared.tile([P, N], U8, name="w2_scale_rows", align_bytes=64, offset=W2_ROWS_AT)
        nc.vector.tensor_copy(
            w2_scale_rows[:].rearrange("p (t m) -> p t m", t=PACK),
            w2_scale_table[:].rearrange("p (m t) -> p t m", t=PACK),
        )
        move_scale_rows(w2_plane, w2_scale_rows)

        x_codes = sb("x_codes", [P, S], U32)
        nc.vector.tensor_copy(x_codes[:], x_table[:].bitcast(U32).indirect(offs_sb[:]))

        w1_grouped = [
            shared.tile([P, 2 * P * PACK], BF16, name="w1_grouped0", align_bytes=64, offset=W2_CODES_AT),
            sb("w1_grouped1", [P, 2 * P * PACK], BF16),
        ]
        w1_codes = sb("w1_codes", [P, H], U32)
        w1_plane = sb("w1_plane", [P, H], U8)
        for a in range(2):
            w1_src = w1_raw[a][:].rearrange("p j (m u e) -> p u m j e", u=2, e=2)
            for u, split in enumerate(VECTOR_COLUMNS[a]):
                w1_dst = w1_grouped[u][:].rearrange("p (e m a j) -> p a m j e", e=2, a=2, j=2)[:, a]
                if split:
                    nc.vector.tensor_copy(w1_dst[:, 0:split], w1_src[:, u, 0:split])
                if split < P:
                    nc.scalar.copy(w1_dst[:, split:P], w1_src[:, u, split:P])
        for t0, t1 in ((0, 1), (1, 2), (2, PACK)):
            nc.vector.quantize_mx(
                out=w1_codes[:, t0 * P : t1 * P].bitcast(FP8X4),
                scales=w1_plane[:, t0 * P : t1 * P],
                in_=w1_grouped[t0 // 2][:, (t0 % 2) * P * PACK : (t0 % 2 + t1 - t0) * P * PACK],
            )

        late = ctx.enter_context(tc.tile_pool(name="late", bufs=1))

        def at(name, shape, dtype, offset):
            return late.tile(shape, dtype, name=name, align_bytes=64, offset=offset)

        def bank(number, shape, dtype=F32):
            return psum.tile(shape, dtype, name="bank%d" % number)

        def first_pass(t, cols, out):
            nc.tensor.matmul_mx(
                out=out,
                lhsT=w1_codes[:, t * P : (t + 1) * P].bitcast(FP8X4),
                lhsT_scale=w1_plane[:, t * P : (t + 1) * P],
                rhs=x_codes[:, cols].bitcast(FP8X4),
                rhs_scale=x_plane[:, cols],
                start=True,
                stop=True,
            )

        def first_product(t, cols, number):
            out = bank(number, [P, cols.stop - cols.start])
            first_pass(t, cols, out[:])
            return out

        silu_y = [at("silu_y%d" % t, [P, S], F32, (0, 5, 4, 6)[t] * 1024) for t in range(PACK)]
        taken = [sb("taken%d" % t, [P, V], F32) for t in range(PACK)]
        y0_sb = sb("y0", [P, S], F32)
        y1_sb = at("y1", [P, S], F32, 1024)

        def entries(v0, v1):
            return take_sb[:, v0 // LIST_ROWS : v1 // LIST_ROWS]

        def look_up(t, v0, v1):
            nc.scalar.activation(taken[t][:, v0:v1], silu_y[t][:].indirect(entries(v0, v1)), COPY)

        def scatter(t, v0, v1, window=None):
            window = d[t] if window is None else window
            nc.vector.tensor_tensor(window[:].indirect(entries(v0, v1)), taken[t][:, v0:v1], wt_sb[:, v0:v1], MULT)

        halves = [slice(0, HALF), slice(HALF, S)]
        y0_banks = [first_product(0, halves[h], h) for h in range(2)]
        for h in range(2):
            nc.scalar.activation(silu_y[0][:, halves[h]], y0_banks[h][:], SILU)
        look_up(0, 0, V // 2)
        look_up(0, V // 2, V)

        for h in range(2):
            nc.vector.tensor_copy(y0_sb[:, halves[h]], y0_banks[h][:])
        scatter(0, 0, V // 2, d_first)
        scatter(0, V // 2, V)
        w2_codes = shared.tile([P, N], U32, name="w2_codes", align_bytes=64, offset=W2_CODES_AT)
        nc.vector.tensor_copy(
            w2_codes[:].rearrange("p (t m) -> p m t", t=PACK),
            w2_table[:].bitcast(U32).rearrange("p (m t) -> p m t", t=PACK),
        )
        y1_cols = (slice(0, S - CHUNK), slice(S - CHUNK, S))
        y1_banks = [bank(2, [P, S - CHUNK])]
        for cols in (slice(0, HALF), slice(HALF, S - CHUNK)):
            first_pass(1, cols, y1_banks[0][:, cols])
        y1_banks.append(first_product(1, y1_cols[1], 0))
        mixed = bank(3, [P, 2, HALF])
        last = bank(7, [P, 2, HALF])
        y_halves = {2: [bank(1, [P, HALF])[:], mixed[:, 0, :]], 3: [mixed[:, 1, :], last[:, 0, :]]}
        for t in range(2, PACK):
            for h in range(2):
                first_pass(t, halves[h], y_halves[t][h])
        for h in range(2):
            nc.scalar.activation(silu_y[1][:, y1_cols[h]], y1_banks[h][:], SILU)
        look_up(1, 0, V)
        scatter(1, 0, V)
        for h in range(2):
            nc.scalar.copy(y1_sb[:, y1_cols[h]], y1_banks[h][:])
        for h in range(2):
            nc.scalar.activation(silu_y[2][:, halves[h]], y_halves[2][h], SILU)
        look_up(2, 0, V)
        scatter(2, 0, V)
        for h in range(2):
            nc.scalar.activation(silu_y[3][:, halves[h]], y_halves[3][h], SILU)
        look_up(3, 0, V)
        scatter(3, 0, V)

        z = at("z", [P, CHUNKS, PACK, CHUNK], BF16, 7680)

        def turned_sum(terms, number):
            out = bank(number, [P, CHUNKS, P])
            for i, src in enumerate(terms):
                for c in range(CHUNKS):
                    nc.tensor.matmul(
                        out[:, c, :],
                        src[c],
                        identity[:],
                        start=(i == 0 and c == 0),
                        stop=(i == len(terms) - 1 and c == CHUNKS - 1),
                        is_transpose=True,
                    )
            return out

        def chunks(tile):
            return [tile[:, c0 : c0 + CHUNK] for c0 in range(0, tile.shape[1], CHUNK)]

        turned = [
            turned_sum((chunks(y0_sb), chunks(d_first), chunks(d[0])), 4),
            turned_sum((chunks(y1_sb), chunks(d[1])), 5),
        ]
        z_turned = [at("z_turned%d" % t, [P, CHUNKS, P], BF16, (4096, 6656)[t]) for t in range(2)]
        for t in range(2):
            nc.scalar.copy(z_turned[t][:], turned[t][:])
        for t in range(2):
            words = (bank(6, [P, HALF])[:], last[:, 1, :])[t] if t == 0 else last[:, 1, :]
            back = words.bitcast(BF16).rearrange("p (c n) -> p c n", n=CHUNK)
            for c in range(CHUNKS):
                nc.tensor.transpose(back[:, c, :], z_turned[t][:, c, :], identity_bf16[:])
            nc.scalar.copy(z[:, :, t, :], back)


        def update(t, c0, c1):
            cols = slice(c0 * CHUNK, c1 * CHUNK)
            nc.vector.tensor_tensor(
                z[:, c0:c1, t, :],
                d[t][:, cols].rearrange("p (c n) -> p c n", n=CHUNK),
                y_halves[t][c0 // 2].rearrange("p (c n) -> p c n", n=CHUNK),
                ADD,
            )

        z_grouped = [at("z_grouped%d" % c, [P, CHUNK * PACK], BF16, (12, 13, 14, 13)[c] * 1024) for c in range(CHUNKS)]
        z_codes = [sb("z_codes%d" % c, [P, CHUNK], U32) for c in range(CHUNKS)]
        z_plane = [sb("z_plane%d" % c, [P, CHUNK], U8) for c in range(CHUNKS)]
        res = sb("res", [P, PACK, S], F32)
        res_grouped = sb("res_grouped", [P, S * PACK], BF16)
        res_codes = sb("res_codes", [P, S], U32)
        res_plane = sb("res_plane", [P, S], U8)
        out_rows = out_0.rearrange("(p t) s -> p t s", t=PACK)

        def group(copy, dst, src):
            copy(
                dst.rearrange("p (n i t) -> p n t i", i=4, t=PACK),
                src.rearrange("p t (n i) -> p n t i", i=4),
            )

        def group_z(c, copy):
            group(copy, z_grouped[c][:], z[:, c])

        def quantize_z(c):
            nc.vector.quantize_mx(out=z_codes[c][:].bitcast(FP8X4), scales=z_plane[c][:], in_=z_grouped[c][:])

        def second_product(c, u, acc):
            for e in range(2):
                t = 2 * u + e
                nc.tensor.matmul_mx(
                    out=acc[:, e, :],
                    lhsT=w2_codes[:, t * P : (t + 1) * P].bitcast(FP8X4),
                    lhsT_scale=w2_plane[:, t * P : (t + 1) * P],
                    rhs=z_codes[c][:].bitcast(FP8X4),
                    rhs_scale=z_plane[c][:],
                    start=True,
                    stop=True,
                )

        def empty(c, u, acc, copy):
            copy(res[:, 2 * u : 2 * u + 2, c * CHUNK : (c + 1) * CHUNK], acc)

        def half_product(first, second, numbers):
            alone = bank(numbers[0], [P, 2, CHUNK])
            both = bank(numbers[1], [P, PACK, CHUNK])
            final = bank(numbers[2], [P, 2, CHUNK])
            second_product(first, 0, alone)
            empty(first, 0, alone[:], nc.scalar.copy)
            second_product(first, 1, both[:, 0:2, :])
            second_product(second, 0, both[:, 2:PACK, :])
            empty(second, 0, both[:, 2:PACK, :], nc.scalar.copy)
            empty(first, 1, both[:, 0:2, :], nc.scalar.copy)
            second_product(second, 1, final)
            empty(second, 1, final[:], nc.vector.tensor_copy)

        def group_result(c, copy):
            group(copy, res_grouped[:, c * CHUNK * PACK : (c + 1) * CHUNK * PACK], res[:, :, c * CHUNK : (c + 1) * CHUNK])

        def quantize_result(c0, c1):
            cols = slice(c0 * CHUNK, c1 * CHUNK)
            nc.vector.quantize_mx(
                out=res_codes[:, cols].bitcast(FP8X4),
                scales=res_plane[:, cols],
                in_=res_grouped[:, c0 * CHUNK * PACK : c1 * CHUNK * PACK],
            )

        update(2, 0, 2)
        update(3, 0, 2)
        update(2, 2, CHUNKS)
        group_z(0, nc.scalar.copy)
        group_z(1, nc.vector.tensor_copy)
        update(3, 2, CHUNKS)
        quantize_z(1)
        quantize_z(0)
        group_z(2, nc.scalar.copy)
        group_z(3, nc.vector.tensor_copy)
        quantize_z(3)
        quantize_z(2)
        half_product(1, 0, (2, 0, 4))
        for u in range(2):
            nc.sync.dma_start(out=out_rows[:, 2 * u : 2 * u + 2, halves[0]], in_=res[:, 2 * u : 2 * u + 2, halves[0]])
        for c, numbers, last_copy in ((3, (6, 1), nc.scalar.copy), (2, (3, 7), nc.vector.tensor_copy)):
            for u, copy in enumerate((nc.scalar.copy, last_copy)):
                acc = bank(numbers[u], [P, 2, CHUNK])
                second_product(c, u, acc)
                empty(c, u, acc[:], copy)
        for u in range(2):
            nc.sync.dma_start(out=out_rows[:, 2 * u : 2 * u + 2, halves[1]], in_=res[:, 2 * u : 2 * u + 2, halves[1]])

        group_result(1, nc.vector.tensor_copy)
        group_result(0, nc.vector.tensor_copy)
        quantize_result(0, 2)
        group_result(3, nc.scalar.copy)
        group_result(2, nc.vector.tensor_copy)
        quantize_result(3, 4)
        quantize_result(2, 3)

        words_out = out_1[0].rearrange("p c r -> p (c r)").bitcast(I32)
        for cols in halves:
            nc.sync.dma_start(out=words_out[:, cols], in_=res_codes[:, cols].bitcast(I32))
        for q in range(P // QUADRANT):
            (nc.scalar, nc.sync)[q // 2].dma_start(
                out=out_2[0, PACK * q : PACK * q + PACK, :].bitcast(I32),
                in_=res_plane[QUADRANT * q : QUADRANT * q + PACK, :].bitcast(I32),
            )
